import numpy as np, ml_dtypes
CORES = [40,64,80,88,96,104,120,144]
N = 8
BF = ml_dtypes.bfloat16
def f(rng, *shape):
    return (rng.standard_normal(shape, dtype=np.float32) * np.exp2(rng.integers(-2, 3, shape[:-1] + (1,)))).astype(BF)
def wide(rng, *shape):
    v = f(rng, *shape).astype(np.float32); k = shape[:-2] + (1, shape[-1])
    return (v * np.exp2(rng.integers(-6, 7, k)) * (rng.random(k) > 0.0625)).astype(BF)
P, NT, W, D = 1024, 64, 256, 64
def order(g):
    return range(N)
def places(ln):
    n = np.asarray(ln).reshape(-1, NT).astype(np.int64) + 1; m = len(n)
    t = np.repeat(np.tile(np.arange(NT), m), n.reshape(-1)).reshape(m, P)
    last = np.zeros((m, P), bool); last[np.arange(m)[:, None], np.add.accumulate(n, 1) - 1] = True
    return t, last
def steps(ln, ds):
    t, last = places(ln); m = len(t); src = np.arange(P) - np.take_along_axis(np.asarray(ds).reshape(m, NT).astype(np.int64), t, 1)
    e = np.zeros((m, P), np.int64); row = np.arange(m)
    for i in range(P):
        j = src[:, i]; e[:, i] = np.where(last[:, i], 0, 1 + np.where(j >= 0, e[row, np.maximum(j, 0)], 0))
    return e
def lengths(rng, at, big):
    n = np.zeros((N, 8, NT), np.int64)
    for r in range(N):
        for g in range(8):
            b = int(big[r, g]); rest = P - NT - b
            v = np.minimum(rng.multinomial(rest, rng.dirichlet(np.where(rng.random(NT - 1) < 0.25, 0.001, 1.0))), D)
            v = v + rng.multivariate_hypergeometric(D - v, rest - int(np.sum(v)))
            n[r, g] = np.insert(v, int(at[r, g]), b)
    return n
def starts(n):
    return np.add.accumulate(n + 1, 2) - n - 1
def distances(rng, n):
    s = starts(n); k = rng.integers(0, 4, n.shape)
    over = rng.integers(np.minimum(s, W - 1) + 1, W + 1)
    return np.where(k == 0, rng.integers(1, 9, n.shape), np.where(k == 3, over, rng.integers(1, W + 1, n.shape)))
def inside(rng, n, d, share):
    s = starts(n); d = np.array(d)
    for g in range(8):
        q = order(g)[0]; m = (d[q, g] > s[q, g]) & (s[q, g] > 0) & (rng.random(NT) < share)
        d[q, g] = np.where(m, rng.integers(1, np.maximum(s[q, g], 1) + 1), d[q, g])
    return d
def fit(n, d):
    d = np.array(d)
    for r in range(N):
        for g in range(8):
            e = []
            for t, (c, k) in enumerate(zip(n[r, g].tolist(), d[r, g].tolist())):
                s = len(e)
                for i in range(s, s + c): e.append(1 + (e[i - k] if i >= k else 0))
                if max(e[s:], default=0) > D:
                    d[r, g, t] = 1; e[s:] = range(1, c + 1)
                e.append(0)
    return d
def pack(rng, n, d):
    return {"ln": n.astype(np.int32), "ds": d.astype(np.int32), "le": f(rng, N, 128, NT)}
def setup_inputs(rng):
    n = lengths(rng, rng.integers(0, NT, (N, 8)), rng.integers(1, D + 1, (N, 8)))
    return pack(rng, n, fit(n, inside(rng, n, distances(rng, n), 0.75)))
def setup_inputs_deep(rng):
    at = np.where(rng.random((N, 8)) < 0.25, rng.choice(np.array([0, NT - 1]), (N, 8)), rng.integers(0, NT, (N, 8)))
    n = lengths(rng, at, np.full((N, 8), D)); d = np.where(rng.random(n.shape) < 0.5, rng.integers(1, 4, n.shape), distances(rng, n))
    d = inside(rng, n, d, 0.75); np.put_along_axis(d, at[:, :, None], 1, 2)
    return pack(rng, n, fit(n, d))
def setup_inputs_hops(rng):
    n = lengths(rng, rng.integers(0, NT, (N, 8)), rng.integers(1, D + 1, (N, 8)))
    return pack(rng, n, fit(n, inside(rng, n, rng.integers(W - 8, W + 1, n.shape), 1.0)))
def setup_inputs_ends(rng):
    at = rng.choice(np.array([0, NT - 1]), (N, 8)); at[:, :2] = 0
    n = lengths(rng, at, rng.integers(2, D + 1, (N, 8))); n[rng.integers(0, N)] = P // NT - 1
    s = starts(n); d = np.choose(rng.integers(0, 6, n.shape), [s * 0 + W, s * 0 + 1, s, s + 1, s + n, n])
    d = inside(rng, n, np.minimum(np.maximum(d, 1), W), 0.5); d[:, 0, 0] = W; d[:, 1, 0] = 1
    return pack(rng, n, fit(n, d))
def setup_inputs_long(rng):
    at = rng.integers(0, NT, (N, 8)); k = rng.integers(P // D, W + 1, (N, 8)); u = rng.integers(0, 3, (N, 8)); k = np.where(u == 0, P // D, np.where(u == 1, W, k))
    for g in range(8):
        q = order(g)[0]; at[q, g] = NT - 1; k[q, g] = rng.integers(P // D, min(W, NT - 1) + 1)
    n = np.zeros((N, 8, NT), np.int64); np.put_along_axis(n, at[:, :, None], P - NT, 2)
    d = rng.integers(1, W + 1, n.shape); np.put_along_axis(d, at[:, :, None], k[:, :, None], 2)
    return pack(rng, n, d)
def setup_inputs_spread(rng):
    d = setup_inputs(rng); d["le"] = wide(rng, N, 128, NT); return d
def check_inputs(d):
    bad = []; a = np.asarray(d["ln"]).astype(np.int64); b = np.asarray(d["ds"]).astype(np.int64)
    if (a < 0).any() or (np.sum(a, 2) + NT != P).any(): bad.append("lengths")
    if (b < 1).any() or (b > W).any(): bad.append("distances")
    if not bad and (steps(a, b) > D).any(): bad.append("steps")
    if not np.isfinite(np.asarray(d["le"]).astype(np.float32)).all(): bad.append("finite")
    return bad
def reference(ln, ds, le):
    y = np.zeros((N, 128, P), BF); t, last = places(ln); t = t.reshape(N, 8, P); last = last.reshape(N, 8, P)
    for g in range(8):
        buf = np.zeros((W + P, 16), BF)
        for r in order(g):
            a = np.ascontiguousarray(le[r, 16 * g:16 * g + 16].T); k = ds[r, g][t[r, g]].tolist(); tk = t[r, g].tolist(); own = last[r, g].tolist()
            for i in range(P):
                buf[W + i] = a[tk[i]] if own[i] else buf[W + i - k[i]]
            y[r, 16 * g:16 * g + 16] = buf[W:].T
            buf[:W] = buf[P:]
    return {"y": y}

@@ -1,0 +1,343 @@
+from concourse.bass import DstId, RemoteDMATransfer
+from concourse.mybir import AluOpType, ActivationFunctionType
+
+OFF = 2047
+BIG = 1344
+POW = [1, 2, 3, 6, 9, 18, 27, 54]
+EARLY = 2
+H = 512
+XV = 352
+B1 = 704
+XY = 416
+XZ = 768
+XC = 352
+SC1 = 720
+BG = 736
+HALF = 528
+SCRATCH = {
+    "xl": ("sbuf", [8, 64], "int32"), "xd": ("sbuf", [8, 64], "int32"),
+    "lastf": ("sbuf", [8, 64], "float16"), "df": ("sbuf", [8, 64], "float16"),
+    "ei": ("sbuf", [8, 128], "int32"), "ee": ("sbuf", [8, 128], "float16"),
+    "ui": ("sbuf", [128, 16], "int32"), "uu": ("sbuf", [128, 16], "int32"),
+    "ma": ("sbuf", [128, 16], "bfloat16"), "mb": ("sbuf", [128, 16], "bfloat16"), "mm": ("sbuf", [128, 512], "bfloat16"),
+    "av": ("sbuf", [128, 64], "bfloat16"), "bv": ("sbuf", [128, 64], "bfloat16"), "ob": ("sbuf", [128, 1], "float32"),
+    "A": ("sbuf", [128, 2 * HALF], "bfloat16"), "B": ("sbuf", [128, 1024], "bfloat16"),
+    "lsc": ("sbuf", [128, 64], "float32"), "lastw": ("sbuf", [128, 4], "uint16"),
+    "f16": ("sbuf", [128, 1024], "float16"), "r16": ("sbuf", [128, 1024], "float16"),
+    "SC": ("sbuf", [128, 1024], "float32"),
+    "t16": ("sbuf", [128, 1024], "float16"), "q16": ("sbuf", [128, 1024], "float16"),
+    "L1": ("sbuf", [128, 64], "uint16"), "L3": ("sbuf", [128, 64], "uint16"),
+    "L9": ("sbuf", [128, 64], "uint16"), "L27": ("sbuf", [128, 64], "uint16"),
+    "TA": ("sbuf", [128, 16], "uint16"), "TB": ("sbuf", [128, 16], "uint16"),
+    "LF": ("sbuf", [128, 64], "uint16"),
+    "hle": ("sbuf", [128, 64], "bfloat16"), "hli": ("sbuf", [128, 16], "uint16"),
+    "yb": ("sbuf", [128, 1024], "bfloat16"),
+    "ps1": ("psum", [128, 512], "float32"), "ps2": ("psum", [128, 512], "float32"),
+}
+for _k in range(4):
+    SCRATCH["W%d" % _k] = ("sbuf", [128, 1344], "float32")
+for _k in range(8):
+    SCRATCH["V%d" % _k] = ("sbuf", [128, 320], "bfloat16")
+    SCRATCH["T%d" % _k] = ("sbuf", [128, 16], "uint16")
+SEMAPHORES = ["v", "s", "pe", "gi", "dln", "dds", "dle", "dy", "loc", "le", "hle", "hli"] + ["ar%d" % k for k in range(8)]
+
+
+def bits(engines):
+    return sum(1 << e for e in engines)
+
+
+def routes(rank, T, topo):
+    src = T.cores[rank]
+    later = list(range(len(T.cores) - 1, rank, -1))
+    straight = [r for r in later if topo.may_write(src, T.cores[r])]
+    cross = [r for r in later if r not in straight]
+    if not cross:
+        return straight, []
+    able = [h for h in topo.cores_of(src) if h != src and T.rank_of(h) is None and topo.may_write(h, T.cores[cross[0]])]
+    able.sort(key=lambda h: (topo.die(h) != topo.die(src), h))
+    n = min(2, len(cross), len(able))
+    eng = topo.engines(src, able[0])
+    inner = [e for e in eng if e not in topo.engines(able[0], T.cores[cross[0]])]
+    return straight, [(able[i], cross[i::n], inner if i else eng) for i in range(n)]
+
+
+def fan(g, T, topo, core, ranks, src, dst, rsem):
+    ids = []
+    for r in ranks:
+        rid, pid = topo.addr(T.cores[r], core)
+        ids.append(DstId(rid=rid, pnc=pid))
+    g.remote_dma_fused([RemoteDMATransfer(dst_ids=ids, dma_engine_mask=topo.mask(core, T.cores[ranks[0]]), remote_sem=rsem,
+                                          srcs=[src], dsts=[dst for _ in ranks])], local_sem=T.sem.loc)
+    return len(topo.engines(core, T.cores[ranks[0]]))
+
+
+def helper(g, core, T, topo):
+    for r in range(len(T.cores)):
+        if core not in topo.cores_of(T.cores[r]):
+            continue
+        for h, ranks, eng in routes(r, T, topo)[1]:
+            if h != core:
+                continue
+            n = 0
+            g.wait_ge(T.sem.hle, len(eng))
+            n += fan(g, T, topo, core, ranks, T.hle[:, :], T["V%d" % r][:, 0:64], T.sem.le)
+            g.wait_ge(T.sem.hli, len(eng))
+            for d in ranks:
+                n += fan(g, T, topo, core, [d], T.hli[:, :], T["T%d" % r][:, :], T.sem["ar%d" % r])
+            g.wait_ge(T.sem.loc, n)
+
+
+def rank_program(g, core, T, topo):
+    rank = T.rank_of(core)
+    if rank is None:
+        helper(g, core, T, topo)
+        return
+    op = AluOpType
+    fn = ActivationFunctionType
+    V, S, PE, SY = g.vector, g.scalar, g.tensor, g.sync
+    queue = {"v": V, "s": S, "pe": PE, "gi": g, "sy": SY}
+    cnt = {}
+    seen = {}
+
+    def need(q, toks):
+        top = {}
+        for sem, val in toks:
+            top[sem] = max(top.get(sem, 0), val)
+        for sem in top:
+            if seen.get((q, sem), 0) < top[sem]:
+                queue[q].wait_ge(T.sem[sem], top[sem])
+                seen[(q, sem)] = top[sem]
+
+    def done(sem, ins, n=1):
+        ins.then_inc(T.sem[sem], n)
+        cnt[sem] = cnt.get(sem, 0) + n
+        return (sem, cnt[sem])
+
+    def gath(q, out, win, lst, deps):
+        need(q, deps)
+        if q == "v":
+            return done("v", V.tensor_copy(out=out, in_=win.indirect(lst)))
+        return done("s", S.activation(out=out, in_=win.indirect(lst), func=fn.Copy))
+
+    def scan(out, data0, data1, initial, op0, op1, deps):
+        need("v", deps)
+        return done("v", V.tensor_tensor_scan(out=out, data0=data0, data1=data1, initial=initial, op0=op0, op1=op1))
+
+    def ts(out, in0, s1, s2, op0, op1, deps):
+        need("v", deps)
+        if op1 is None:
+            return done("v", V.tensor_scalar(out=out, in0=in0, scalar1=s1, scalar2=None, op0=op0))
+        return done("v", V.tensor_scalar(out=out, in0=in0, scalar1=s1, scalar2=s2, op0=op0, op1=op1))
+
+    mine = T["V%d" % rank]
+    straight, relays = routes(rank, T, topo)
+    last = not straight and not relays
+    early_rank = rank < EARLY
+    ln = done("dln", SY.dma_start(out=T.xl[:, :], in_=T.ln[:, :]), 16)
+    ds = done("dds", S.dma_start(out=T.xd[:, :], in_=T.ds[:, :]), 16)
+    le = done("dle", SY.dma_start(out=mine[:, 0:64], in_=T.le[:, :]), 16)
+    flag = {"allow_small_or_imprecise_dtypes": True}
+    add = float(OFF - BIG)
+    ident = {}
+
+    def roots(i):
+        ident[i] = done("gi", g.iota(T["W%d" % i][:, 0:320], [[1, 320]], -OFF, 0, **flag))
+
+    ui = done("gi", g.iota(T.ui[:, :], [[1, 16]], 128, -1))
+    ei = done("gi", g.iota(T.ei[:, :], [[1, 8], [0, 16]], 0, -1))
+    bh = done("gi", g.iota(T.B[:, 0:1024 - BG], [[0, 1024 - BG]], 0, 0, **flag))
+    bg = done("gi", g.iota(T.B[:, 1024 - BG:BG], [[0, 2 * BG - 1024]], 0, 0, **flag))
+    roots(0)
+    a1 = done("v", V.memset(T.A[:, 0:HALF], 1.0))
+    uu = ts(T.uu[:, :], T.ui[:, :], 15, None, op.bitwise_and, None, [ui])
+    ma = ts(T.ma[:, :], T.uu[:, :], 0.0, -8192.0, op.is_equal, op.mult, [uu])
+    mb = ts(T.mb[:, :], T.uu[:, :], 1.0, float(BIG), op.is_equal, op.mult, [uu])
+    ee = ts(T.ee[:, :], T.ei[:, :], 0.0, None, op.is_equal, None, [ei])
+    need("v", [ma, mb])
+    mtok = {16: done("v", V.tensor_tensor(out=T.mm[:, 0:16], in0=T.ma[:, :], in1=T.mb[:, :], op=op.add))}
+
+    def widen(to):
+        w = max(mtok)
+        while w < to:
+            n = min(w, to - w)
+            need("s", [mtok[w]])
+            mtok[w + n] = done("s", S.activation(out=T.mm[:, w:w + n], in_=T.mm[:, 0:n], func=fn.Copy))
+            w += n
+
+    need("s", [a1])
+    a2 = done("s", S.activation(out=T.A[:, HALF:2 * HALF], in_=T.A[:, 0:HALF], func=fn.Copy))
+    widen(64)
+    last16 = T.mb[:, 0:1]
+
+    def relist(src, tmp, n, deps):
+        return scan(tmp, T.mm[:, 0:n], src, 0.0, op.add, op.max, deps + [mtok[min(w for w in mtok if w >= n)], mb])
+
+    def offs(out, picked, deps):
+        return ts(out, picked, last16, add, op.add, op.add, deps)
+
+    lastf = scan(T.lastf[:, :], T.A[0:8, 16:80], T.xl[:, :], -1.0, op.add, op.add, [ln, a1])
+    need("pe", [lastf, ee])
+    p1 = done("pe", PE.matmul(T.ps1[:, 0:64], T.ee[:, :], T.lastf[:, :], True, True))
+    need("v", [ds])
+    df = done("v", V.tensor_copy(out=T.df[:, :], in_=T.xd[:, :]))
+    av63 = done("v", V.memset(T.av[:, 63:64], 1.0))
+    ob = ts(T.ob[:, :], T.mb[:, 0:1], add, None, op.add, None, [mb])
+    need("pe", [df])
+    p2 = done("pe", PE.matmul(T.ps2[:, 0:64], T.ee[:, :], T.df[:, :], True, True))
+    need("s", [p2])
+    avt = done("s", S.activation(out=T.av[:, 0:63], in_=T.ps2[:, 1:64], func=fn.Identity, bias=1.0, scale=-1.0))
+    bvt = done("s", S.activation(out=T.bv[:, :], in_=T.ps2[:, 0:64], func=fn.Copy))
+    need("s", [a2])
+    first = done("s", S.activation(out=T.A[:, 15:16], in_=T.ps2[:, 0:1], func=fn.Identity, bias=1.0, scale=-1.0))
+    need("s", [bh])
+    b0 = done("s", S.activation(out=T.B[:, BG:1024], in_=T.B[:, 0:1024 - BG], func=fn.Copy))
+    widen(512)
+    t = relist(T.ps1[:, 0:64], T.lsc[:, :], 64, [p1])
+    lw = ts(T.lastw[:, :], T.lsc[:, 15:64:16], last16, -float(BIG), op.add, op.add, [t])
+    need("v", [lw, avt, av63, a2])
+    sca = done("v", V.tensor_copy(out=T.A[:, 16:1040].indirect(T.lastw[:, 0:4]), in_=T.av[:, :]))
+    need("v", [bvt, b0, bg])
+    scb = done("v", V.tensor_copy(out=T.B[:, 0:1024].indirect(T.lastw[:, 0:4]), in_=T.bv[:, :]))
+    h = scan(T.f16[:, :], T.A[:, 15:1039], T.B[:, :], float(319 - OFF), op.add, op.add, [sca, scb, first])
+    need("s", [h])
+    fcopy = done("s", S.activation(out=T.W0[:, 320:320 + SC1], in_=T.f16[:, 0:SC1], func=fn.Copy))
+    need("gi", [h])
+    gcopy = done("gi", g.affine_select(T.W0[:, 320 + SC1:1344], T.f16[:, SC1:1024], [[0, 1024 - SC1]], op.is_equal, 0.0, 0, 0))
+    for i in (1, 2, 3):
+        roots(i)
+    z0 = done("gi", g.iota(T.V0[:, 64:320], [[0, 256]], 0, 0, **flag))
+    relist(T.f16[:, 0:512], T.r16[:, 0:512], 512, [h])
+    t = relist(T.f16[:, 512:1024], T.r16[:, 512:1024], 512, [h])
+    l1 = offs(T.L1[:, :], T.r16[:, 15:1024:16], [t])
+    need("v", [fcopy, gcopy, ident[0]])
+    code = done("v", V.tensor_copy(out=T.W0[:, 320:1344].indirect(T.lastw[:, 0:4]), in_=T.W0[:, 0:64]))
+
+    base = 320
+    LIST = {1: T.L1, 3: T.L3, 9: T.L9, 27: T.L27}
+    WIN = {k: T["W%d" % (i % 4)] for i, k in enumerate(POW)}
+    made = {1: [(0, 1024, code)]}
+    listed = {1: [(0, 1024, l1)]}
+    readers = {}
+
+    def after(where, a, b):
+        return [x[2] for x in where if x[0] < b and a < x[1]]
+
+    def whole(k):
+        return [ident[POW.index(k) % 4]] + after(made[k], 0, 1024)
+
+    def jump(q, a_, b_, c0, c1):
+        k = a_ + b_
+        i = POW.index(k)
+        old = readers.get(POW[i - 4], []) if i >= 4 else []
+        deps = [ident[POW.index(a_) % 4]] + after(made[a_], 0, c1) + after(listed[b_], c0, c1) + old
+        t = gath(q, WIN[k][:, base + c0:base + c1], WIN[a_][:, 0:base + c1], LIST[b_][:, c0 // 16:c1 // 16], deps)
+        readers.setdefault(a_, []).append(t)
+        made.setdefault(k, []).append((c0, c1, t))
+
+    def pick(k, c0, c1):
+        return relist(WIN[k][:, base + c0:base + c1], T.SC[:, c0:c1], c1 - c0, after(made[k], c0, c1))
+
+    def lists(q, k, c0, c1, toks):
+        out, src = LIST[k][:, c0 // 16:c1 // 16], T.SC[:, c0 + 15:c1:16]
+        if q == "v":
+            t = offs(out, src, toks)
+        else:
+            need("s", toks + [ob])
+            t = done("s", S.activation(out=out, in_=src, func=fn.Identity, bias=T.ob[:, 0:1]))
+        listed.setdefault(k, []).append((c0, c1, t))
+
+    def tail(k, lst, c0, out, deps):
+        deps = deps + whole(k)
+        win = WIN[k][:, :]
+        a = gath("v", T.t16[:, 768:896], win, lst[:, c0:c0 + 8], deps)
+        b = gath("s", T.t16[:, 896:1024], win, lst[:, c0 + 8:c0 + 16], deps)
+        t = relist(T.t16[:, 768:1024], T.q16[:, 768:1024], 256, [a, b])
+        return offs(out, T.q16[:, 783:1024:16], [t])
+
+    jump("s", 1, 1, 0, 256)
+    jump("v", 1, 1, 256, 512)
+    jump("s", 1, 1, 512, 768)
+    jump("v", 1, 1, 768, 1024)
+    lt = None
+    for k in (1, 3, 9):
+        if k == 9 and early_rank:
+            jump("s", 18, 9, XC, 1024)
+            jump("v", 18, 9, 0, XC)
+            t = relist(WIN[18][:, base + 768:base + 1024], T.SC[:, 768:1024], 256, after(made[18], 768, 1024))
+            lt = offs(T.TA[:, :], T.SC[:, 783:1024:16], [t])
+            lt = tail(27, T.TA, 0, T.TB[:, :], [lt])
+            lt = tail(27, T.TB, 0, T.LF[:, 48:64], [lt])
+        else:
+            jump("s", 2 * k, k, XV, H)
+            jump("v", 2 * k, k, 0, XV)
+            jump("s", 2 * k, k, H, B1)
+            jump("s", 2 * k, k, B1, 1024)
+        lists("s", 3 * k, 0, H, [pick(3 * k, 0, H)])
+        jump("s", 3 * k, 3 * k, 0, XY)
+        t = [pick(3 * k, H, B1), pick(3 * k, B1, 1024)]
+        jump("v", 3 * k, 3 * k, XY, H)
+        lists("v", 3 * k, H, 1024, t)
+        jump("v", 3 * k, 3 * k, H, XZ)
+        jump("s", 3 * k, 3 * k, XZ, 1024)
+    fb = whole(54) + after(listed[27], 0, 1024)
+    if not early_rank and not last:
+        lt = tail(54, T.L27, 48, T.LF[:, 48:64], fb)
+
+    loc = 0
+    for what in () if last else ("le", "list"):
+        early = what == "le"
+        need("gi", [le] if early else [lt])
+        src = mine[:, 0:64] if early else T.LF[:, 48:64]
+        calls = []
+        if relays:
+            calls.append((relays[0], None))
+        if straight:
+            calls.append((None, straight if early else straight[:1]))
+        calls += [(x, None) for x in relays[1:]]
+        if straight[1:] and not early:
+            calls.append((None, straight[1:]))
+        for relay, ranks in calls:
+            if relay:
+                h, _, eng = relay
+                rid, pid = topo.addr(h, core)
+                g.remote_dma(out_ap=T.hle[:, :] if early else T.hli[:, :], in_ap=src,
+                             remote_sem=T.sem.hle if early else T.sem.hli, local_sem=T.sem.loc,
+                             pid=pid, routing_id=rid, dma_engine_mask=bits(eng))
+                loc += len(eng)
+            else:
+                dst = mine[:, 0:64] if early else T["T%d" % rank][:, :]
+                loc += fan(g, T, topo, core, ranks, src, dst, T.sem.le if early else T.sem["ar%d" % rank])
+
+    n = 1024 if last else 768
+    m = n // 2
+    FB = WIN[54][:, :]
+    tv = gath("v", T.t16[:, 0:m], FB, T.L27[:, 0:m // 16], fb)
+    ts_ = gath("s", T.t16[:, m:n], FB, T.L27[:, m // 16:n // 16], fb)
+    relist(T.t16[:, 0:m], T.q16[:, 0:m], m, [tv])
+    t = relist(T.t16[:, m:n], T.q16[:, m:n], m, [ts_])
+    lr = offs(T.LF[:, 0:n // 16], T.q16[:, 15:n:16], [t])
+
+    prev = [z0]
+    total_le = 0
+    got = []
+    for k in range(rank):
+        hop = [c for c in routes(k, T, topo)[1] if rank in c[1]]
+        n = len(topo.engines(hop[0][0] if hop else T.cores[k], core))
+        total_le += n
+        got.append(("ar%d" % k, n))
+    for k in range(rank):
+        w, nx, lst = T["V%d" % k], T["V%d" % (k + 1)], T["T%d" % k]
+        deps = prev + [("le", total_le), got[k]]
+        a = gath("v", nx[:, 64:192], w[:, 0:320], lst[:, 0:8], deps)
+        b = gath("s", nx[:, 192:320], w[:, 0:320], lst[:, 8:16], deps)
+        prev = [a, b]
+
+    win = mine[:, 0:320]
+    deps = prev + [le, lr] + ([] if last else [lt])
+    for q, issue, a, b in (("v", "sy", 0, 320), ("s", "sy", 512, 832), ("v", "sy", 320, 512), ("s", "s", 832, 1024)):
+        t = gath(q, T.yb[:, a:b], win, T.LF[:, a // 16:b // 16], deps)
+        need(issue, [t])
+        done("dy", queue[issue].dma_start(out=T.y[:, a:b], in_=T.yb[:, a:b]), 16)
+    need("sy", [(s, cnt[s]) for s in ("dy", "v", "s", "pe", "gi", "dln", "dds", "dle")])
+    if loc:
+        g.wait_ge(T.sem.loc, loc)

@@ -1,45 +1,37 @@
 from concourse.bass import DstId, RemoteDMATransfer
 from concourse.mybir import AluOpType, ActivationFunctionType
 
-OFF = 2047
-BIG = 1344
-POW = [1, 2, 3, 6, 9, 18, 27, 54]
-EARLY = 2
-H = 512
-XV = 352
-B1 = 704
-XY = 416
-XZ = 768
-XC = 352
-SC1 = 720
-BG = 736
-HALF = 528
+BASE = 320
+CUT = 512
+SHARE = 0.5
+BYDMA = 4
+ORDER = ("+A0 vA +U0 A1 sU A2/9 +A2 B1 T1 B2/5 vA T2/1 +U2 P3 Q3 P4 sU Q4/6 +A4 B3 T3 B4 +B4 T4 sA T9@4 +T9>4 "
+         "P5 sB Q5/6 B5/0 sT P6/8 Q6 T5 B6 T6 +T6 R7 T7 +R7 vT T8 +T8 sR R8/6 vT! +R8 sR!")
+LAST = ORDER
+STORE = [0, 512, 1024]
 SCRATCH = {
     "xl": ("sbuf", [8, 64], "int32"), "xd": ("sbuf", [8, 64], "int32"),
-    "lastf": ("sbuf", [8, 64], "float16"), "df": ("sbuf", [8, 64], "float16"),
-    "ei": ("sbuf", [8, 128], "int32"), "ee": ("sbuf", [8, 128], "float16"),
-    "ui": ("sbuf", [128, 16], "int32"), "uu": ("sbuf", [128, 16], "int32"),
-    "ma": ("sbuf", [128, 16], "bfloat16"), "mb": ("sbuf", [128, 16], "bfloat16"), "mm": ("sbuf", [128, 512], "bfloat16"),
-    "av": ("sbuf", [128, 64], "bfloat16"), "bv": ("sbuf", [128, 64], "bfloat16"), "ob": ("sbuf", [128, 1], "float32"),
-    "A": ("sbuf", [128, 2 * HALF], "bfloat16"), "B": ("sbuf", [128, 1024], "bfloat16"),
-    "lsc": ("sbuf", [128, 64], "float32"), "lastw": ("sbuf", [128, 4], "uint16"),
-    "f16": ("sbuf", [128, 1024], "float16"), "r16": ("sbuf", [128, 1024], "float16"),
-    "SC": ("sbuf", [128, 1024], "float32"),
-    "t16": ("sbuf", [128, 1024], "float16"), "q16": ("sbuf", [128, 1024], "float16"),
-    "L1": ("sbuf", [128, 64], "uint16"), "L3": ("sbuf", [128, 64], "uint16"),
-    "L9": ("sbuf", [128, 64], "uint16"), "L27": ("sbuf", [128, 64], "uint16"),
-    "TA": ("sbuf", [128, 16], "uint16"), "TB": ("sbuf", [128, 16], "uint16"),
+    "one": ("sbuf", [8, 64], "float16"), "lastf": ("sbuf", [8, 64], "float16"), "pd": ("sbuf", [8, 72], "float16"),
+    "ji": ("sbuf", [8, 144], "int32"), "Y": ("sbuf", [8, 144], "float16"), "EB": ("sbuf", [8, 128], "float16"),
+    "r8": ("sbuf", [8, 64], "float16"),
+    "ui": ("sbuf", [128, 32], "int32"), "uu": ("sbuf", [128, 32], "int32"),
+    "mq": ("sbuf", [128, 16], "float32"), "bias": ("sbuf", [128, 4], "float32"), "col": ("sbuf", [128, 2], "float32"),
+    "ramp": ("sbuf", [128, BASE], "bfloat16"), "Z": ("sbuf", [128, 144], "bfloat16"),
+    "bv": ("sbuf", [128, 64], "bfloat16"),
+    "A": ("sbuf", [128, 1024], "bfloat16"), "B": ("sbuf", [128, 1024], "bfloat16"),
+    "lastw": ("sbuf", [128, 4], "uint16"),
     "LF": ("sbuf", [128, 64], "uint16"),
     "hle": ("sbuf", [128, 64], "bfloat16"), "hli": ("sbuf", [128, 16], "uint16"),
     "yb": ("sbuf", [128, 1024], "bfloat16"),
-    "ps1": ("psum", [128, 512], "float32"), "ps2": ("psum", [128, 512], "float32"),
 }
-for _k in range(4):
-    SCRATCH["W%d" % _k] = ("sbuf", [128, 1344], "float32")
+for _k in range(10):
+    SCRATCH["W%d" % _k] = ("sbuf", [128, BASE + 1024], "bfloat16")
+    SCRATCH["L%d" % _k] = ("sbuf", [128, 64], "uint16")
 for _k in range(8):
     SCRATCH["V%d" % _k] = ("sbuf", [128, 320], "bfloat16")
     SCRATCH["T%d" % _k] = ("sbuf", [128, 16], "uint16")
-SEMAPHORES = ["v", "s", "pe", "gi", "dln", "dds", "dle", "dy", "loc", "le", "hle", "hli"] + ["ar%d" % k for k in range(8)]
+    SCRATCH["ps%d" % _k] = ("psum", [128, 512], "float32")
+SEMAPHORES = ["v", "s", "pe", "gi", "dln", "dds", "dle", "dr", "dy", "loc", "le", "hle", "hli"] + ["ar%d" % k for k in range(8)]
 
 
 def bits(engines):
@@ -129,159 +121,132 @@ def rank_program(g, core, T, topo):
             return done("v", V.tensor_scalar(out=out, in0=in0, scalar1=s1, scalar2=None, op0=op0))
         return done("v", V.tensor_scalar(out=out, in0=in0, scalar1=s1, scalar2=s2, op0=op0, op1=op1))
 
+    def tt(out, in0, in1, op0, deps):
+        need("v", deps)
+        return done("v", V.tensor_tensor(out=out, in0=in0, in1=in1, op=op0))
+
+    def act(out, in_, scale, bias, deps):
+        need("s", deps)
+        return done("s", S.activation(out=out, in_=in_, func=fn.Identity, bias=bias, scale=scale))
+
+    def relist(out, pick, src, c0, c1, deps):
+        need("pe", deps)
+        for r in range(16):
+            m = PE.matmul(out, pick(r), src[:, c0 + r:c1:16], r == 0, r == 15)
+        return done("pe", m)
+
     mine = T["V%d" % rank]
+    W = [T["W%d" % k] for k in range(10)]
     straight, relays = routes(rank, T, topo)
     last = not straight and not relays
-    early_rank = rank < EARLY
     ln = done("dln", SY.dma_start(out=T.xl[:, :], in_=T.ln[:, :]), 16)
     ds = done("dds", S.dma_start(out=T.xd[:, :], in_=T.ds[:, :]), 16)
     le = done("dle", SY.dma_start(out=mine[:, 0:64], in_=T.le[:, :]), 16)
     flag = {"allow_small_or_imprecise_dtypes": True}
-    add = float(OFF - BIG)
-    ident = {}
-
-    def roots(i):
-        ident[i] = done("gi", g.iota(T["W%d" % i][:, 0:320], [[1, 320]], -OFF, 0, **flag))
-
-    ui = done("gi", g.iota(T.ui[:, :], [[1, 16]], 128, -1))
-    ei = done("gi", g.iota(T.ei[:, :], [[1, 8], [0, 16]], 0, -1))
-    bh = done("gi", g.iota(T.B[:, 0:1024 - BG], [[0, 1024 - BG]], 0, 0, **flag))
-    bg = done("gi", g.iota(T.B[:, 1024 - BG:BG], [[0, 2 * BG - 1024]], 0, 0, **flag))
-    roots(0)
-    a1 = done("v", V.memset(T.A[:, 0:HALF], 1.0))
-    uu = ts(T.uu[:, :], T.ui[:, :], 15, None, op.bitwise_and, None, [ui])
-    ma = ts(T.ma[:, :], T.uu[:, :], 0.0, -8192.0, op.is_equal, op.mult, [uu])
-    mb = ts(T.mb[:, :], T.uu[:, :], 1.0, float(BIG), op.is_equal, op.mult, [uu])
-    ee = ts(T.ee[:, :], T.ei[:, :], 0.0, None, op.is_equal, None, [ei])
-    need("v", [ma, mb])
-    mtok = {16: done("v", V.tensor_tensor(out=T.mm[:, 0:16], in0=T.ma[:, :], in1=T.mb[:, :], op=op.add))}
-
-    def widen(to):
-        w = max(mtok)
-        while w < to:
-            n = min(w, to - w)
-            need("s", [mtok[w]])
-            mtok[w + n] = done("s", S.activation(out=T.mm[:, w:w + n], in_=T.mm[:, 0:n], func=fn.Copy))
-            w += n
-
-    need("s", [a1])
-    a2 = done("s", S.activation(out=T.A[:, HALF:2 * HALF], in_=T.A[:, 0:HALF], func=fn.Copy))
-    widen(64)
-    last16 = T.mb[:, 0:1]
-
-    def relist(src, tmp, n, deps):
-        return scan(tmp, T.mm[:, 0:n], src, 0.0, op.add, op.max, deps + [mtok[min(w for w in mtok if w >= n)], mb])
-
-    def offs(out, picked, deps):
-        return ts(out, picked, last16, add, op.add, op.add, deps)
-
-    lastf = scan(T.lastf[:, :], T.A[0:8, 16:80], T.xl[:, :], -1.0, op.add, op.add, [ln, a1])
-    need("pe", [lastf, ee])
-    p1 = done("pe", PE.matmul(T.ps1[:, 0:64], T.ee[:, :], T.lastf[:, :], True, True))
+    ui = done("gi", g.iota(T.ui[:, 0:4], [[-1, 4]], 16, 1))
+    ramp = done("gi", g.iota(T.ramp[:, :], [[1, BASE]], -64, 0, **flag))
+    one = done("v", V.memset(T.one[:, :], 1.0))
+    p64 = done("v", V.memset(T.pd[:, 64:72], 0.0))
+    uu = ts(T.uu[:, 0:4], T.ui[:, 0:4], 15, None, op.bitwise_and, None, [ui])
+    yc = ts(T.col[:, 0:1], T.ui[:, 0:1], 16.0, -304.0, op.mult, op.add, [ui])
+    mq = ts(T.mq[:, 0:4], T.uu[:, 0:4], 0.0, None, op.is_equal, None, [uu])
+    zc = tt(T.col[:, 1:2], T.ui[:, 0:1], T.uu[:, 0:1], op.subtract, [uu])
+    hi, lo, run = T.mq[:, 0:1], T.mq[:, 1:2], T.mq[:, 2:3]
+    y = ts(T.Y[:, :], T.ramp[0:8, 0:144], T.col[0:8, 0:1], None, op.is_equal, None, [ramp, yc])
+    bias = ts(T.bias[:, :], T.ramp[:, 65:69], hi, 256.0, op.mult, op.mult, [ramp, mq])
+    k0 = act(T.A[:, 0:256], T.ramp[:, 0:256], 0.0, run, [mq, ramp])
+    need("gi", [k0])
+    keep = done("gi", g.affine_select(T.A[:, 256:512], T.A[:, 0:256], [[0, 256]], op.is_equal, 0.0, 0, 0))
+    lastf = scan(T.lastf[:, :], T.one[:, :], T.xl[:, :], -1.0, op.add, op.add, [ln, one])
+    p1 = relist(T.ps0[:, 0:4], lambda r: T.Y[:, 16 - r:144 - r], T.lastf, 0, 64, [lastf, y])
+    eb = tt(T.EB[:, :], T.Y[:, 16:144], T.Y[:, 14:142], op.subtract, [y])
     need("v", [ds])
-    df = done("v", V.tensor_copy(out=T.df[:, :], in_=T.xd[:, :]))
-    av63 = done("v", V.memset(T.av[:, 63:64], 1.0))
-    ob = ts(T.ob[:, :], T.mb[:, 0:1], add, None, op.add, None, [mb])
-    need("pe", [df])
-    p2 = done("pe", PE.matmul(T.ps2[:, 0:64], T.ee[:, :], T.df[:, :], True, True))
-    need("s", [p2])
-    avt = done("s", S.activation(out=T.av[:, 0:63], in_=T.ps2[:, 1:64], func=fn.Identity, bias=1.0, scale=-1.0))
-    bvt = done("s", S.activation(out=T.bv[:, :], in_=T.ps2[:, 0:64], func=fn.Copy))
-    need("s", [a2])
-    first = done("s", S.activation(out=T.A[:, 15:16], in_=T.ps2[:, 0:1], func=fn.Identity, bias=1.0, scale=-1.0))
-    need("s", [bh])
-    b0 = done("s", S.activation(out=T.B[:, BG:1024], in_=T.B[:, 0:1024 - BG], func=fn.Copy))
-    widen(512)
-    t = relist(T.ps1[:, 0:64], T.lsc[:, :], 64, [p1])
-    lw = ts(T.lastw[:, :], T.lsc[:, 15:64:16], last16, -float(BIG), op.add, op.add, [t])
-    need("v", [lw, avt, av63, a2])
-    sca = done("v", V.tensor_copy(out=T.A[:, 16:1040].indirect(T.lastw[:, 0:4]), in_=T.av[:, :]))
-    need("v", [bvt, b0, bg])
-    scb = done("v", V.tensor_copy(out=T.B[:, 0:1024].indirect(T.lastw[:, 0:4]), in_=T.bv[:, :]))
-    h = scan(T.f16[:, :], T.A[:, 15:1039], T.B[:, :], float(319 - OFF), op.add, op.add, [sca, scb, first])
-    need("s", [h])
-    fcopy = done("s", S.activation(out=T.W0[:, 320:320 + SC1], in_=T.f16[:, 0:SC1], func=fn.Copy))
-    need("gi", [h])
-    gcopy = done("gi", g.affine_select(T.W0[:, 320 + SC1:1344], T.f16[:, SC1:1024], [[0, 1024 - SC1]], op.is_equal, 0.0, 0, 0))
-    for i in (1, 2, 3):
-        roots(i)
-    z0 = done("gi", g.iota(T.V0[:, 64:320], [[0, 256]], 0, 0, **flag))
-    relist(T.f16[:, 0:512], T.r16[:, 0:512], 512, [h])
-    t = relist(T.f16[:, 512:1024], T.r16[:, 512:1024], 512, [h])
-    l1 = offs(T.L1[:, :], T.r16[:, 15:1024:16], [t])
-    need("v", [fcopy, gcopy, ident[0]])
-    code = done("v", V.tensor_copy(out=T.W0[:, 320:1344].indirect(T.lastw[:, 0:4]), in_=T.W0[:, 0:64]))
+    pd = done("v", V.tensor_copy(out=T.pd[:, 0:64], in_=T.xd[:, :]))
+    need("pe", [pd, p64, eb])
+    PE.matmul(T.ps1[:, 0:65], T.EB[:, :], T.pd[:, 0:65], True, False)
+    PE.matmul(T.ps1[:, 1:65], T.Y[:, 14:142], T.pd[:, 0:64], False, False)
+    p2 = done("pe", PE.matmul(T.ps1[:, 1:65], T.Y[:, 15:143], T.ramp[0:8, 0:64], False, True))
+    bg = []
+    for j in (2, 3):
+        bg.append(act(T.B[:, 256 * j:256 * j + 256], T.ramp[:, 64:BASE], lo, T.bias[:, j:j + 1], [bias]))
+    for j in (0, 1):
+        bg.append(ts(T.B[:, 256 * j:256 * j + 256], T.ramp[:, 64:BASE], lo, T.bias[:, j:j + 1], op.mult, op.add, [bias]))
+    bv = act(T.bv[:, :], T.ps1[:, 1:65], 1.0, 0.0, [p2])
+    need("v", [p1])
+    lw = done("v", V.tensor_copy(out=T.lastw[:, :], in_=T.ps0[:, 0:4]))
+    z = ts(T.Z[:, :], T.ramp[:, 0:144], T.col[:, 1:2], -65.0, op.subtract, op.is_equal, [zc])
+    need("v", [lw, bv] + bg)
+    sc = done("v", V.tensor_copy(out=T.B[:, :].indirect(T.lastw[:, 0:4]), in_=T.bv[:, :]))
+    h0 = scan(W[0][:, BASE:BASE + 512], T.A[:, 0:512], T.B[:, 0:512], T.ps1[:, 0:1], op.mult, op.add, [sc, keep])
+    root = {0: act(W[0][:, 0:BASE], T.ramp[:, :], lo, 0.0, [mq, ramp])}
+    h1 = scan(W[0][:, BASE + 512:BASE + 1024], T.A[:, 0:512], T.B[:, 512:1024], W[0][:, BASE + 511:BASE + 512],
+              op.mult, op.add, [h0])
+    need("gi", [root[0]])
+    need("sy", [root[0]])
+    for k in range(1, 8):
+        if k < 8 - BYDMA:
+            root[k] = done("gi", g.affine_select(W[k][:, 0:BASE], W[0][:, 0:BASE], [[0, BASE]], op.is_equal, 0.0, 0, 0))
+        else:
+            done("dr", SY.dma_start(out=W[k][:, 0:BASE], in_=W[0][:, 0:BASE]), 16)
+            root[k] = ("dr", 16 * BYDMA)
+    zero = done("gi", g.iota(T.V0[:, 64:320], [[0, 256]], 0, 0, **flag))
 
-    base = 320
-    LIST = {1: T.L1, 3: T.L3, 9: T.L9, 27: T.L27}
-    WIN = {k: T["W%d" % (i % 4)] for i, k in enumerate(POW)}
-    made = {1: [(0, 1024, code)]}
-    listed = {1: [(0, 1024, l1)]}
-    readers = {}
+    span = {"A": (0, CUT), "B": (CUT, 768), "T": (768, 1024), "U": (CUT, 1024), "R": (0, 768), "W": (0, 1024),
+            "P": (0, CUT // 2), "Q": (CUT // 2, CUT)}
+    made = {0: [(0, 512, h0), (512, 1024, h1)]}
+    lists = []
+    bank = [2]
+    free = {}
+    pend = {}
 
     def after(where, a, b):
-        return [x[2] for x in where if x[0] < b and a < x[1]]
+        return [x[-1] for x in where if x[0] < b and a < x[1]]
 
-    def whole(k):
-        return [ident[POW.index(k) % 4]] + after(made[k], 0, 1024)
+    def tolist(c, k, name):
+        a, b = span[c]
+        i = bank[0]
+        bank[0] = 2 + (i - 1) % 6
+        ps = T["ps%d" % i][:, 0:(b - a) // 16]
+        t = relist(ps, lambda r: T.Z[:, 15 - r:143 - r], W[k], BASE + a, BASE + b, after(made[k], a, b) + [z] + free.get(i, []))
+        pend[c] = (i, ps, name, t)
 
-    def jump(q, a_, b_, c0, c1):
-        k = a_ + b_
-        i = POW.index(k)
-        old = readers.get(POW[i - 4], []) if i >= 4 else []
-        deps = [ident[POW.index(a_) % 4]] + after(made[a_], 0, c1) + after(listed[b_], c0, c1) + old
-        t = gath(q, WIN[k][:, base + c0:base + c1], WIN[a_][:, 0:base + c1], LIST[b_][:, c0 // 16:c1 // 16], deps)
-        readers.setdefault(a_, []).append(t)
-        made.setdefault(k, []).append((c0, c1, t))
-
-    def pick(k, c0, c1):
-        return relist(WIN[k][:, base + c0:base + c1], T.SC[:, c0:c1], c1 - c0, after(made[k], c0, c1))
-
-    def lists(q, k, c0, c1, toks):
-        out, src = LIST[k][:, c0 // 16:c1 // 16], T.SC[:, c0 + 15:c1:16]
+    def take(q, c, final):
+        a, b = span[c]
+        i, ps, k, t = pend.pop(c)
+        buf = T.LF if final else T["L%d" % k]
+        out = buf[:, a // 16:b // 16]
         if q == "v":
-            t = offs(out, src, toks)
+            t = ts(out, ps, 64.0, None, op.add, None, [t])
         else:
-            need("s", toks + [ob])
-            t = done("s", S.activation(out=out, in_=src, func=fn.Identity, bias=T.ob[:, 0:1]))
-        listed.setdefault(k, []).append((c0, c1, t))
+            t = act(out, ps, 1.0, 64.0, [t])
+        free[i] = [t]
+        lists.append((a, b, k, t))
+        return t
 
-    def tail(k, lst, c0, out, deps):
-        deps = deps + whole(k)
-        win = WIN[k][:, :]
-        a = gath("v", T.t16[:, 768:896], win, lst[:, c0:c0 + 8], deps)
-        b = gath("s", T.t16[:, 896:1024], win, lst[:, c0 + 8:c0 + 16], deps)
-        t = relist(T.t16[:, 768:1024], T.q16[:, 768:1024], 256, [a, b])
-        return offs(out, T.q16[:, 783:1024:16], [t])
+    def jump(c, k, src, n):
+        a, b = span[c]
+        m = a + 32 * n if n is not None else (a + b) // 2
+        for q, c0, c1 in (("s", m, b), ("v", a, m)):
+            if c0 == c1:
+                continue
+            j = max(x[2] for x in lists if x[0] <= c0 < x[1])
+            deps = [root[src]] + after([x for x in lists if x[2] == j], c0, c1) + after(made[src], 0, c1)
+            t = gath(q, W[k][:, BASE + c0:BASE + c1], W[src][:, 0:BASE + c1], T["L%d" % j][:, c0 // 16:c1 // 16], deps)
+            made.setdefault(k, []).append((c0, c1, t))
 
-    jump("s", 1, 1, 0, 256)
-    jump("v", 1, 1, 256, 512)
-    jump("s", 1, 1, 512, 768)
-    jump("v", 1, 1, 768, 1024)
-    lt = None
-    for k in (1, 3, 9):
-        if k == 9 and early_rank:
-            jump("s", 18, 9, XC, 1024)
-            jump("v", 18, 9, 0, XC)
-            t = relist(WIN[18][:, base + 768:base + 1024], T.SC[:, 768:1024], 256, after(made[18], 768, 1024))
-            lt = offs(T.TA[:, :], T.SC[:, 783:1024:16], [t])
-            lt = tail(27, T.TA, 0, T.TB[:, :], [lt])
-            lt = tail(27, T.TB, 0, T.LF[:, 48:64], [lt])
+    final = []
+    for w in (LAST if last else ORDER).split():
+        if w[0] in "vs":
+            t = take(w[0], w[1], w[-1] == "!")
+            if w[-1] == "!":
+                final.append(t)
+                if w[1] == "T":
+                    lt = t
+        elif w[0] == "+":
+            tolist(w[1], int(w[2]), int(w[-1]))
         else:
-            jump("s", 2 * k, k, XV, H)
-            jump("v", 2 * k, k, 0, XV)
-            jump("s", 2 * k, k, H, B1)
-            jump("s", 2 * k, k, B1, 1024)
-        lists("s", 3 * k, 0, H, [pick(3 * k, 0, H)])
-        jump("s", 3 * k, 3 * k, 0, XY)
-        t = [pick(3 * k, H, B1), pick(3 * k, B1, 1024)]
-        jump("v", 3 * k, 3 * k, XY, H)
-        lists("v", 3 * k, H, 1024, t)
-        jump("v", 3 * k, 3 * k, H, XZ)
-        jump("s", 3 * k, 3 * k, XZ, 1024)
-    fb = whole(54) + after(listed[27], 0, 1024)
-    if not early_rank and not last:
-        lt = tail(54, T.L27, 48, T.LF[:, 48:64], fb)
+            k = int(w[1])
+            jump(w[0], k, int(w[3]) if "@" in w else k - 1, int(w.split("/")[1]) if "/" in w else None)
 
     loc = 0
     for what in () if last else ("le", "list"):
@@ -308,16 +273,7 @@ def rank_program(g, core, T, topo):
                 dst = mine[:, 0:64] if early else T["T%d" % rank][:, :]
                 loc += fan(g, T, topo, core, ranks, src, dst, T.sem.le if early else T.sem["ar%d" % rank])
 
-    n = 1024 if last else 768
-    m = n // 2
-    FB = WIN[54][:, :]
-    tv = gath("v", T.t16[:, 0:m], FB, T.L27[:, 0:m // 16], fb)
-    ts_ = gath("s", T.t16[:, m:n], FB, T.L27[:, m // 16:n // 16], fb)
-    relist(T.t16[:, 0:m], T.q16[:, 0:m], m, [tv])
-    t = relist(T.t16[:, m:n], T.q16[:, m:n], m, [ts_])
-    lr = offs(T.LF[:, 0:n // 16], T.q16[:, 15:n:16], [t])
-
-    prev = [z0]
+    prev = [zero]
     total_le = 0
     got = []
     for k in range(rank):
@@ -333,11 +289,11 @@ def rank_program(g, core, T, topo):
         prev = [a, b]
 
     win = mine[:, 0:320]
-    deps = prev + [le, lr] + ([] if last else [lt])
-    for q, issue, a, b in (("v", "sy", 0, 320), ("s", "sy", 512, 832), ("v", "sy", 320, 512), ("s", "s", 832, 1024)):
-        t = gath(q, T.yb[:, a:b], win, T.LF[:, a // 16:b // 16], deps)
-        need(issue, [t])
-        done("dy", queue[issue].dma_start(out=T.y[:, a:b], in_=T.yb[:, a:b]), 16)
-    need("sy", [(s, cnt[s]) for s in ("dy", "v", "s", "pe", "gi", "dln", "dds", "dle")])
+    deps = prev + [le] + final
+    for a, b in zip(STORE, STORE[1:]):
+        m = (a + b) // 64 * 32
+        need("sy", [gath(q, T.yb[:, c0:c1], win, T.LF[:, c0 // 16:c1 // 16], deps) for q, c0, c1 in (("v", a, m), ("s", m, b))])
+        done("dy", SY.dma_start(out=T.y[:, a:b], in_=T.yb[:, a:b]), 16)
+    need("sy", [(s, cnt[s]) for s in ("dy", "v", "s", "pe", "gi", "dln", "dds", "dle", "dr") if s in cnt])
     if loc:
         g.wait_ge(T.sem.loc, loc)

@@ -7,11 +7,14 @@ SHARE = 0.5
 BYDMA = 4
 ORDER = ("+A0 vA +U0 A1 sU A2/9 +A2 B1 T1 B2/5 vA T2/1 +U2 P3 Q3 P4 sU Q4/6 +A4 B3 T3 B4 +B4 T4 sA T9@4 +T9>4 "
          "P5 sB Q5/6 B5/0 sT P6/8 Q6 T5 B6 T6 +T6 R7 T7 +R7 vT T8 +T8 sR R8/6 vT! +R8 sR!")
-LAST = ORDER
+LAST = ("+A0 vA +U0 A1 sU A2/9 +A2 B1 T1 B2/5 vA T2/1 +U2 P3 Q3 P4 sU Q4/6 +A4 B3 T3 B4 vA T4/2 +U4 "
+        "P5 Q5 P6 sU Q6/6 +A6 B5 T5 B6 vA T6/2 +U6 P7 Q7 P8 sU Q8/6 +A8 B7 T7 B8 T8 +U8 vA! vU!")
+LATE = 2
+LIST = 1.5
 STORE = [0, 512, 1024]
 SCRATCH = {
     "xl": ("sbuf", [8, 64], "int32"), "xd": ("sbuf", [8, 64], "int32"),
-    "one": ("sbuf", [8, 64], "float16"), "lastf": ("sbuf", [8, 64], "float16"), "pd": ("sbuf", [8, 72], "float16"),
+    "one": ("sbuf", [8, 144], "float16"), "lastf": ("sbuf", [8, 64], "float16"), "pd": ("sbuf", [8, 72], "float16"),
     "ji": ("sbuf", [8, 144], "int32"), "Y": ("sbuf", [8, 144], "float16"), "EB": ("sbuf", [8, 128], "float16"),
     "r8": ("sbuf", [8, 64], "float16"),
     "ui": ("sbuf", [128, 32], "int32"), "uu": ("sbuf", [128, 32], "int32"),
@@ -28,7 +31,9 @@ for _k in range(10):
     SCRATCH["W%d" % _k] = ("sbuf", [128, BASE + 1024], "bfloat16")
     SCRATCH["L%d" % _k] = ("sbuf", [128, 64], "uint16")
 for _k in range(8):
-    SCRATCH["V%d" % _k] = ("sbuf", [128, 320], "bfloat16")
+    SCRATCH["V%d" % _k] = ("sbuf", [128, 448], "bfloat16")
+    SCRATCH["P%d" % _k] = ("sbuf", [128, 320], "bfloat16")
+    SCRATCH["C%d" % _k] = ("sbuf", [128, 16], "uint16")
     SCRATCH["T%d" % _k] = ("sbuf", [128, 16], "uint16")
     SCRATCH["ps%d" % _k] = ("psum", [128, 512], "float32")
 SEMAPHORES = ["v", "s", "pe", "gi", "dln", "dds", "dle", "dr", "dy", "loc", "le", "hle", "hli"] + ["ar%d" % k for k in range(8)]
@@ -53,13 +58,49 @@ def routes(rank, T, topo):
     return straight, [(able[i], cross[i::n], inner if i else eng) for i in range(n)]
 
 
+def runs(rank, T, topo):
+    best = None
+    for cut in range(1 << max(rank - 1, 0)):
+        starts = [k for k in range(rank) if k == 0 or cut >> (k - 1) & 1]
+        parts = list(zip(starts, starts[1:] + [rank]))
+        if any(b - a > 3 for a, b in parts):
+            continue
+        calls = []
+        for a, b in parts:
+            come = [0 if topo.may_write(T.cores[k], T.cores[rank]) else LATE for k in range(a, b)]
+            before = [("D", x, y - 1) for x, y in parts if y == a]
+            if b - a > 1:
+                calls += [(("P", a, k), [("P", a, k - 1)] if k > a else [], come[k - a]) for k in range(a, b)]
+                calls += [(("C", a, b - 1), [("P", a, b - 1)], 0), (("D", a, b - 1), before + [("C", a, b - 1)], 0)]
+            else:
+                calls.append((("D", a, a), before, come[0]))
+        end, order, now = {}, [], 0
+        while calls:
+            ready = [(max([now, c[2]] + [end[d] + (LIST if c[0][0] == "C" else 0) for d in c[1]]), c[0][0] == "D", c)
+                     for c in calls if all(d in end for d in c[1])]
+            t, _, c = min(ready)
+            calls.remove(c)
+            order.append(c[0])
+            now = t + (0.25 if c[0][0] == "C" else 0.5)
+            end[c[0]] = now + 0.5
+        key = (max(end.values(), default=0), len(order))
+        if best is None or key < best[0]:
+            best = (key, order)
+    return best[1]
+
+
+def letters(k, rank, T, topo):
+    a = min(c[1] for c in runs(rank, T, topo) if c[1] <= k <= c[2])
+    return T["V%d" % a][:, 0:64] if a == k else T["V%d" % a][:, 256 + 64 * (k - a):320 + 64 * (k - a)]
+
+
 def fan(g, T, topo, core, ranks, src, dst, rsem):
     ids = []
     for r in ranks:
         rid, pid = topo.addr(T.cores[r], core)
         ids.append(DstId(rid=rid, pnc=pid))
     g.remote_dma_fused([RemoteDMATransfer(dst_ids=ids, dma_engine_mask=topo.mask(core, T.cores[ranks[0]]), remote_sem=rsem,
-                                          srcs=[src], dsts=[dst for _ in ranks])], local_sem=T.sem.loc)
+                                          srcs=[src], dsts=[dst(r) for r in ranks])], local_sem=T.sem.loc)
     return len(topo.engines(core, T.cores[ranks[0]]))
 
 
@@ -72,10 +113,10 @@ def helper(g, core, T, topo):
                 continue
             n = 0
             g.wait_ge(T.sem.hle, len(eng))
-            n += fan(g, T, topo, core, ranks, T.hle[:, :], T["V%d" % r][:, 0:64], T.sem.le)
+            n += fan(g, T, topo, core, ranks, T.hle[:, :], lambda d: letters(r, d, T, topo), T.sem.le)
             g.wait_ge(T.sem.hli, len(eng))
             for d in ranks:
-                n += fan(g, T, topo, core, [d], T.hli[:, :], T["T%d" % r][:, :], T.sem["ar%d" % r])
+                n += fan(g, T, topo, core, [d], T.hli[:, :], lambda d: T["T%d" % r][:, :], T.sem["ar%d" % r])
             g.wait_ge(T.sem.loc, n)
 
 
@@ -144,25 +185,26 @@ def rank_program(g, core, T, topo):
     le = done("dle", SY.dma_start(out=mine[:, 0:64], in_=T.le[:, :]), 16)
     flag = {"allow_small_or_imprecise_dtypes": True}
     ui = done("gi", g.iota(T.ui[:, 0:4], [[-1, 4]], 16, 1))
-    ramp = done("gi", g.iota(T.ramp[:, :], [[1, BASE]], -64, 0, **flag))
+    ramp = done("gi", g.iota(T.ramp[:, 64:BASE], [[1, 256]], 0, 0, **flag))
     one = done("v", V.memset(T.one[:, :], 1.0))
+    need("gi", [one])
+    y = done("gi", g.affine_select(T.Y[:, :], T.one[:, :], [[1, 144]], op.is_equal, 0.0, -16, -16))
+    ramp0 = done("gi", g.iota(T.ramp[:, 0:64], [[1, 64]], -64, 0, **flag))
     p64 = done("v", V.memset(T.pd[:, 64:72], 0.0))
     uu = ts(T.uu[:, 0:4], T.ui[:, 0:4], 15, None, op.bitwise_and, None, [ui])
-    yc = ts(T.col[:, 0:1], T.ui[:, 0:1], 16.0, -304.0, op.mult, op.add, [ui])
     mq = ts(T.mq[:, 0:4], T.uu[:, 0:4], 0.0, None, op.is_equal, None, [uu])
     zc = tt(T.col[:, 1:2], T.ui[:, 0:1], T.uu[:, 0:1], op.subtract, [uu])
     hi, lo, run = T.mq[:, 0:1], T.mq[:, 1:2], T.mq[:, 2:3]
-    y = ts(T.Y[:, :], T.ramp[0:8, 0:144], T.col[0:8, 0:1], None, op.is_equal, None, [ramp, yc])
     bias = ts(T.bias[:, :], T.ramp[:, 65:69], hi, 256.0, op.mult, op.mult, [ramp, mq])
-    k0 = act(T.A[:, 0:256], T.ramp[:, 0:256], 0.0, run, [mq, ramp])
+    k0 = act(T.A[:, 0:256], T.ramp[:, 64:BASE], 0.0, run, [mq, ramp])
     need("gi", [k0])
     keep = done("gi", g.affine_select(T.A[:, 256:512], T.A[:, 0:256], [[0, 256]], op.is_equal, 0.0, 0, 0))
-    lastf = scan(T.lastf[:, :], T.one[:, :], T.xl[:, :], -1.0, op.add, op.add, [ln, one])
+    lastf = scan(T.lastf[:, :], T.one[:, 0:64], T.xl[:, :], -1.0, op.add, op.add, [ln, one])
     p1 = relist(T.ps0[:, 0:4], lambda r: T.Y[:, 16 - r:144 - r], T.lastf, 0, 64, [lastf, y])
-    eb = tt(T.EB[:, :], T.Y[:, 16:144], T.Y[:, 14:142], op.subtract, [y])
     need("v", [ds])
     pd = done("v", V.tensor_copy(out=T.pd[:, 0:64], in_=T.xd[:, :]))
-    need("pe", [pd, p64, eb])
+    eb = tt(T.EB[:, :], T.Y[:, 16:144], T.Y[:, 14:142], op.subtract, [y])
+    need("pe", [pd, p64, eb, ramp0])
     PE.matmul(T.ps1[:, 0:65], T.EB[:, :], T.pd[:, 0:65], True, False)
     PE.matmul(T.ps1[:, 1:65], T.Y[:, 14:142], T.pd[:, 0:64], False, False)
     p2 = done("pe", PE.matmul(T.ps1[:, 1:65], T.Y[:, 15:143], T.ramp[0:8, 0:64], False, True))
@@ -174,11 +216,11 @@ def rank_program(g, core, T, topo):
     bv = act(T.bv[:, :], T.ps1[:, 1:65], 1.0, 0.0, [p2])
     need("v", [p1])
     lw = done("v", V.tensor_copy(out=T.lastw[:, :], in_=T.ps0[:, 0:4]))
-    z = ts(T.Z[:, :], T.ramp[:, 0:144], T.col[:, 1:2], -65.0, op.subtract, op.is_equal, [zc])
+    z = ts(T.Z[:, :], T.ramp[:, 64:208], T.col[:, 1:2], -1.0, op.subtract, op.is_equal, [zc])
     need("v", [lw, bv] + bg)
     sc = done("v", V.tensor_copy(out=T.B[:, :].indirect(T.lastw[:, 0:4]), in_=T.bv[:, :]))
     h0 = scan(W[0][:, BASE:BASE + 512], T.A[:, 0:512], T.B[:, 0:512], T.ps1[:, 0:1], op.mult, op.add, [sc, keep])
-    root = {0: act(W[0][:, 0:BASE], T.ramp[:, :], lo, 0.0, [mq, ramp])}
+    root = {0: act(W[0][:, 0:BASE], T.ramp[:, :], lo, 0.0, [mq, ramp0])}
     h1 = scan(W[0][:, BASE + 512:BASE + 1024], T.A[:, 0:512], T.B[:, 512:1024], W[0][:, BASE + 511:BASE + 512],
               op.mult, op.add, [h0])
     need("gi", [root[0]])
@@ -270,7 +312,7 @@ def rank_program(g, core, T, topo):
                              pid=pid, routing_id=rid, dma_engine_mask=bits(eng))
                 loc += len(eng)
             else:
-                dst = mine[:, 0:64] if early else T["T%d" % rank][:, :]
+                dst = (lambda d: letters(rank, d, T, topo)) if early else (lambda d: T["T%d" % rank][:, :])
                 loc += fan(g, T, topo, core, ranks, src, dst, T.sem.le if early else T.sem["ar%d" % rank])
 
     prev = [zero]
@@ -281,12 +323,29 @@ def rank_program(g, core, T, topo):
         n = len(topo.engines(hop[0][0] if hop else T.cores[k], core))
         total_le += n
         got.append(("ar%d" % k, n))
-    for k in range(rank):
-        w, nx, lst = T["V%d" % k], T["V%d" % (k + 1)], T["T%d" % k]
-        deps = prev + [("le", total_le), got[k]]
-        a = gath("v", nx[:, 64:192], w[:, 0:320], lst[:, 0:8], deps)
-        b = gath("s", nx[:, 192:320], w[:, 0:320], lst[:, 8:16], deps)
-        prev = [a, b]
+    chain = runs(rank, T, topo)
+    names = {}
+    for what, a, k in chain:
+        if what == "P" and k > a:
+            names[k] = act(T["P%d" % k][:, 0:64], T.ramp[:, 64 * (k - a):64 * (k - a) + 64], lo, T.bias[:, 0:1], [])
+    step = {}
+    joined = [c for c in chain if c[0] == "C"]
+    for what, a, k in chain:
+        if what == "C":
+            step[what, k] = [ts(T["C%d" % k][:, :], step["ps", k][0], 64.0, None, op.add, None, [step["ps", k][1]])]
+            continue
+        if what == "P":
+            win, out, lst = (W[0] if k == a else T["P%d" % k])[:, 0:320], T["P%d" % (k + 1)], T["T%d" % k]
+            deps = [got[k]] + ([root[0]] if k == a else [names[k]] + step["P", k - 1])
+        else:
+            win, out, lst = T["V%d" % a][:, 0:320 + 64 * (k - a)], T["V%d" % (k + 1)], T["C%d" % k if k > a else "T%d" % k]
+            deps = prev + [("le", total_le)] + (step["C", k] if k > a else [got[k]])
+        step[what, k] = [gath("v", out[:, 64:192], win, lst[:, 0:8], deps), gath("s", out[:, 192:320], win, lst[:, 8:16], deps)]
+        if what == "D":
+            prev = step[what, k]
+        elif ("C", a, k) in chain:
+            ps = T["ps%d" % joined.index(("C", a, k))][:, 0:16]
+            step["ps", k] = (ps, relist(ps, lambda r: T.Z[:, 15 - r:143 - r], out, 64, 320, step[what, k]))
 
     win = mine[:, 0:320]
     deps = prev + [le] + final

@@ -5,20 +5,19 @@ BASE = 320
 CUT = 512
 SHARE = 0.5
 BYDMA = 4
-ORDER = ("+A0 vA +U0 A1 sU A2/9 +A2 B1 T1 B2/5 vA T2/1 +U2 P3 Q3 P4 sU Q4/6 +A4 B3 T3 B4 +B4 T4 sA T9@4 +T9>4 "
-         "P5 sB Q5/6 B5/0 sT P6/8 Q6 T5 B6 T6 +T6 R7 T7 +R7 vT T8 +T8 sR R8/6 vT! +R8 sR!")
+ORDER = ("+A0 sA +U0 P1 Q1/5 sU P2/5 Q2 +A2 B1 T1 B2 sA T2/6 +U2 P3 Q3 P4 vU Q4/3 +A4 B3 T3 B4/5 +B4 sA T4 P5 T9@4 +T9>4 "
+         "vB Q5/3 P6 B5 vT Q6/3 T5 B6 T6 +T6 R7/16 T7/0 vT +R7 T8 +T8 vR vT! R8/8 +R8 sR!")
 LAST = ("+A0 vA +U0 A1 sU A2/9 +A2 B1 T1 B2/5 vA T2/1 +U2 P3 Q3 P4 sU Q4/6 +A4 B3 T3 B4 vA T4/2 +U4 "
         "P5 Q5 P6 sU Q6/6 +A6 B5 T5 B6 vA T6/2 +U6 P7 Q7 P8 sU Q8/6 +A8 B7 T7 B8 T8 +U8 vA! vU!")
 LATE = 2
-LIST = 1.5
+LIST = 1.0
 STORE = [0, 512, 1024]
 SCRATCH = {
     "xl": ("sbuf", [8, 64], "int32"), "xd": ("sbuf", [8, 64], "int32"),
-    "one": ("sbuf", [8, 144], "float16"), "lastf": ("sbuf", [8, 64], "float16"), "pd": ("sbuf", [8, 72], "float16"),
-    "ji": ("sbuf", [8, 144], "int32"), "Y": ("sbuf", [8, 144], "float16"), "EB": ("sbuf", [8, 128], "float16"),
-    "r8": ("sbuf", [8, 64], "float16"),
-    "ui": ("sbuf", [128, 32], "int32"), "uu": ("sbuf", [128, 32], "int32"),
-    "mq": ("sbuf", [128, 16], "float32"), "bias": ("sbuf", [128, 4], "float32"), "col": ("sbuf", [128, 2], "float32"),
+    "one": ("sbuf", [128, 256], "bfloat16"), "lastf": ("sbuf", [8, 64], "float16"), "pd": ("sbuf", [8, 144], "float16"),
+    "Y": ("sbuf", [8, 144], "float16"),
+    "ui": ("sbuf", [128, 16], "int32"), "uu": ("sbuf", [128, 16], "int32"),
+    "mq": ("sbuf", [128, 16], "float32"), "col": ("sbuf", [128, 1], "float32"),
     "ramp": ("sbuf", [128, BASE], "bfloat16"), "Z": ("sbuf", [128, 144], "bfloat16"),
     "bv": ("sbuf", [128, 64], "bfloat16"),
     "A": ("sbuf", [128, 1024], "bfloat16"), "B": ("sbuf", [128, 1024], "bfloat16"),
@@ -53,9 +52,7 @@ def routes(rank, T, topo):
     able = [h for h in topo.cores_of(src) if h != src and T.rank_of(h) is None and topo.may_write(h, T.cores[cross[0]])]
     able.sort(key=lambda h: (topo.die(h) != topo.die(src), h))
     n = min(2, len(cross), len(able))
-    eng = topo.engines(src, able[0])
-    inner = [e for e in eng if e not in topo.engines(able[0], T.cores[cross[0]])]
-    return straight, [(able[i], cross[i::n], inner if i else eng) for i in range(n)]
+    return straight, [(able[i], cross[i::n], topo.engines(src, able[i])) for i in range(n)]
 
 
 def runs(rank, T, topo):
@@ -184,42 +181,41 @@ def rank_program(g, core, T, topo):
     ds = done("dds", S.dma_start(out=T.xd[:, :], in_=T.ds[:, :]), 16)
     le = done("dle", SY.dma_start(out=mine[:, 0:64], in_=T.le[:, :]), 16)
     flag = {"allow_small_or_imprecise_dtypes": True}
-    ui = done("gi", g.iota(T.ui[:, 0:4], [[-1, 4]], 16, 1))
-    ramp = done("gi", g.iota(T.ramp[:, 64:BASE], [[1, 256]], 0, 0, **flag))
+    ui = done("gi", g.iota(T.ui[:, :], [[1793, 2], [2048, 2], [256, 4]], 30976, -2048))
     one = done("v", V.memset(T.one[:, :], 1.0))
     need("gi", [one])
-    y = done("gi", g.affine_select(T.Y[:, :], T.one[:, :], [[1, 144]], op.is_equal, 0.0, -16, -16))
+    y = done("gi", g.affine_select(T.Y[:, :], T.one[0:8, 0:144], [[1, 144]], op.is_equal, 0.0, -16, -16))
     ramp0 = done("gi", g.iota(T.ramp[:, 0:64], [[1, 64]], -64, 0, **flag))
-    p64 = done("v", V.memset(T.pd[:, 64:72], 0.0))
-    uu = ts(T.uu[:, 0:4], T.ui[:, 0:4], 15, None, op.bitwise_and, None, [ui])
-    mq = ts(T.mq[:, 0:4], T.uu[:, 0:4], 0.0, None, op.is_equal, None, [uu])
-    zc = tt(T.col[:, 1:2], T.ui[:, 0:1], T.uu[:, 0:1], op.subtract, [uu])
-    hi, lo, run = T.mq[:, 0:1], T.mq[:, 1:2], T.mq[:, 2:3]
-    bias = ts(T.bias[:, :], T.ramp[:, 65:69], hi, 256.0, op.mult, op.mult, [ramp, mq])
-    k0 = act(T.A[:, 0:256], T.ramp[:, 64:BASE], 0.0, run, [mq, ramp])
-    need("gi", [k0])
-    keep = done("gi", g.affine_select(T.A[:, 256:512], T.A[:, 0:256], [[0, 256]], op.is_equal, 0.0, 0, 0))
-    lastf = scan(T.lastf[:, :], T.one[:, 0:64], T.xl[:, :], -1.0, op.add, op.add, [ln, one])
+    p64 = done("v", V.memset(T.pd[:, :], 0.0))
+    uu = ts(T.uu[:, :], T.ui[:, :], 32767, None, op.bitwise_and, None, [ui])
+    ramp = scan(T.ramp[:, 64:BASE], T.one[:, :], T.one[:, :], -1.0, op.mult, op.add, [one])
+    mq = ts(T.mq[:, :], T.uu[:, :], 30720.0, 0.0, op.subtract, op.max, [uu])
+    lo, run = T.mq[:, 8:9], T.mq[:, 12:13]
+    lastf = scan(T.lastf[:, :], T.one[0:8, 0:64], T.xl[:, :], -1.0, op.add, op.add, [ln, one])
     p1 = relist(T.ps0[:, 0:4], lambda r: T.Y[:, 16 - r:144 - r], T.lastf, 0, 64, [lastf, y])
     need("v", [ds])
     pd = done("v", V.tensor_copy(out=T.pd[:, 0:64], in_=T.xd[:, :]))
-    eb = tt(T.EB[:, :], T.Y[:, 16:144], T.Y[:, 14:142], op.subtract, [y])
-    need("pe", [pd, p64, eb, ramp0])
-    PE.matmul(T.ps1[:, 0:65], T.EB[:, :], T.pd[:, 0:65], True, False)
+    nd = act(T.pd[:, 72:136], T.xd[:, :], -1.0, 0.0, [ds, p64])
+    need("pe", [pd, nd, ramp0])
+    PE.matmul(T.ps1[:, 0:65], T.Y[:, 14:142], T.pd[:, 72:137], True, False)
+    PE.matmul(T.ps1[:, 0:65], T.Y[:, 16:144], T.pd[:, 0:65], False, False)
     PE.matmul(T.ps1[:, 1:65], T.Y[:, 14:142], T.pd[:, 0:64], False, False)
     p2 = done("pe", PE.matmul(T.ps1[:, 1:65], T.Y[:, 15:143], T.ramp[0:8, 0:64], False, True))
     bg = []
     for j in (2, 3):
-        bg.append(act(T.B[:, 256 * j:256 * j + 256], T.ramp[:, 64:BASE], lo, T.bias[:, j:j + 1], [bias]))
+        bg.append(act(T.B[:, 256 * j:256 * j + 256], T.ramp[:, 64:BASE], lo, T.mq[:, j:j + 1], [mq, ramp]))
     for j in (0, 1):
-        bg.append(ts(T.B[:, 256 * j:256 * j + 256], T.ramp[:, 64:BASE], lo, T.bias[:, j:j + 1], op.mult, op.add, [bias]))
+        bg.append(ts(T.B[:, 256 * j:256 * j + 256], T.ramp[:, 64:BASE], lo, T.mq[:, j:j + 1], op.mult, op.add, [mq, ramp]))
     bv = act(T.bv[:, :], T.ps1[:, 1:65], 1.0, 0.0, [p2])
+    zc = tt(T.col[:, 0:1], T.uu[:, 0:1], T.ui[:, 0:1], op.subtract, [uu])
+    keep = [ts(T.A[:, 0:256], T.one[:, :], run, None, op.mult, None, [mq])]
     need("v", [p1])
     lw = done("v", V.tensor_copy(out=T.lastw[:, :], in_=T.ps0[:, 0:4]))
-    z = ts(T.Z[:, :], T.ramp[:, 64:208], T.col[:, 1:2], -1.0, op.subtract, op.is_equal, [zc])
+    keep.append(ts(T.A[:, 256:512], T.one[:, :], run, None, op.mult, None, [mq]))
     need("v", [lw, bv] + bg)
     sc = done("v", V.tensor_copy(out=T.B[:, :].indirect(T.lastw[:, 0:4]), in_=T.bv[:, :]))
-    h0 = scan(W[0][:, BASE:BASE + 512], T.A[:, 0:512], T.B[:, 0:512], T.ps1[:, 0:1], op.mult, op.add, [sc, keep])
+    z = ts(T.Z[:, :], T.ramp[:, 49:193], 2048.0, T.col[:, 0:1], op.mult, op.is_equal, [zc, ramp0])
+    h0 = scan(W[0][:, BASE:BASE + 512], T.A[:, 0:512], T.B[:, 0:512], T.ps1[:, 0:1], op.mult, op.add, [sc] + keep)
     root = {0: act(W[0][:, 0:BASE], T.ramp[:, :], lo, 0.0, [mq, ramp0])}
     h1 = scan(W[0][:, BASE + 512:BASE + 1024], T.A[:, 0:512], T.B[:, 512:1024], W[0][:, BASE + 511:BASE + 512],
               op.mult, op.add, [h0])
@@ -295,25 +291,15 @@ def rank_program(g, core, T, topo):
         early = what == "le"
         need("gi", [le] if early else [lt])
         src = mine[:, 0:64] if early else T.LF[:, 48:64]
-        calls = []
         if relays:
-            calls.append((relays[0], None))
+            ids = [DstId(rid=a[0], pnc=a[1]) for a in (topo.addr(h, core) for h, _, _ in relays)]
+            g.remote_dma_fused([RemoteDMATransfer(dst_ids=ids, dma_engine_mask=bits(relays[0][2]), srcs=[src],
+                                                  dsts=[T.hle[:, :] if early else T.hli[:, :] for _ in relays],
+                                                  remote_sem=T.sem.hle if early else T.sem.hli)], local_sem=T.sem.loc)
+            loc += len(relays[0][2])
         if straight:
-            calls.append((None, straight if early else straight[:1]))
-        calls += [(x, None) for x in relays[1:]]
-        if straight[1:] and not early:
-            calls.append((None, straight[1:]))
-        for relay, ranks in calls:
-            if relay:
-                h, _, eng = relay
-                rid, pid = topo.addr(h, core)
-                g.remote_dma(out_ap=T.hle[:, :] if early else T.hli[:, :], in_ap=src,
-                             remote_sem=T.sem.hle if early else T.sem.hli, local_sem=T.sem.loc,
-                             pid=pid, routing_id=rid, dma_engine_mask=bits(eng))
-                loc += len(eng)
-            else:
-                dst = (lambda d: letters(rank, d, T, topo)) if early else (lambda d: T["T%d" % rank][:, :])
-                loc += fan(g, T, topo, core, ranks, src, dst, T.sem.le if early else T.sem["ar%d" % rank])
+            dst = (lambda d: letters(rank, d, T, topo)) if early else (lambda d: T["T%d" % rank][:, :])
+            loc += fan(g, T, topo, core, straight, src, dst, T.sem.le if early else T.sem["ar%d" % rank])
 
     prev = [zero]
     total_le = 0
@@ -327,7 +313,7 @@ def rank_program(g, core, T, topo):
     names = {}
     for what, a, k in chain:
         if what == "P" and k > a:
-            names[k] = act(T["P%d" % k][:, 0:64], T.ramp[:, 64 * (k - a):64 * (k - a) + 64], lo, T.bias[:, 0:1], [])
+            names[k] = act(T["P%d" % k][:, 0:64], T.ramp[:, 64 * (k - a):64 * (k - a) + 64], lo, T.mq[:, 0:1], [])
     step = {}
     joined = [c for c in chain if c[0] == "C"]
     for what, a, k in chain:

@@ -5,10 +5,10 @@ BASE = 320
 CUT = 512
 SHARE = 0.5
 BYDMA = 4
-ORDER = ("+A0 sA +U0 P1 Q1/5 sU P2/5 Q2 +A2 B1 T1 B2 sA T2/6 +U2 P3 Q3 P4 vU Q4/3 +A4 B3 T3 B4/5 +B4 sA T4 P5 T9@4 +T9>4 "
-         "vB Q5/3 P6 B5 vT Q6/3 T5 B6 T6 +T6 R7/16 T7/0 vT +R7 T8 +T8 vR vT! R8/8 +R8 sR!")
-LAST = ("+A0 vA +U0 A1 sU A2/9 +A2 B1 T1 B2/5 vA T2/1 +U2 P3 Q3 P4 sU Q4/6 +A4 B3 T3 B4 vA T4/2 +U4 "
-        "P5 Q5 P6 sU Q6/6 +A6 B5 T5 B6 vA T6/2 +U6 P7 Q7 P8 sU Q8/6 +A8 B7 T7 B8 T8 +U8 vA! vU!")
+FIB = ("+A0 vA +U0 sU A1/11 +A1 U1/9 +U1 " + "".join("A%d sA +A%d U%d vU +U%d " % (k, k, k, k) for k in range(2, 6))
+       + "A6 sA U6 vU ")
+ORDER = FIB + "T7 +T7 R7 vT +R7 T8 +T8 vR vT! R8/8 +R8 sR!"
+LAST = FIB + "A7 +A7 U7 +U7 sA A8 +A8 vU U8 +U8 sA! vU!"
 LATE = 2
 LIST = 1.0
 STORE = [0, 512, 1024]

from concourse.bass import DstId, RemoteDMATransfer
from concourse.mybir import AluOpType, ActivationFunctionType

BASE = 320
CUT = 512
SHARE = 0.5
BYDMA = 4
FIB = ("+A0 vA +U0 sU A1/11 +A1 U1/9 +U1 " + "".join("A%d sA +A%d U%d vU +U%d " % (k, k, k, k) for k in range(2, 6))
       + "A6 sA U6 vU ")
ORDER = FIB + "T7 +T7 R7 vT +R7 T8 +T8 vR vT! R8/8 +R8 sR!"
LAST = FIB + "A7 +A7 U7 +U7 sA A8 +A8 vU U8 +U8 sA! vU!"
LATE = 2
LIST = 1.0
STORE = [0, 512, 1024]
SCRATCH = {
    "xl": ("sbuf", [8, 64], "int32"), "xd": ("sbuf", [8, 64], "int32"),
    "one": ("sbuf", [128, 256], "bfloat16"), "lastf": ("sbuf", [8, 64], "float16"), "pd": ("sbuf", [8, 144], "float16"),
    "Y": ("sbuf", [8, 144], "float16"),
    "ui": ("sbuf", [128, 16], "int32"), "uu": ("sbuf", [128, 16], "int32"),
    "mq": ("sbuf", [128, 16], "float32"), "col": ("sbuf", [128, 1], "float32"),
    "ramp": ("sbuf", [128, BASE], "bfloat16"), "Z": ("sbuf", [128, 144], "bfloat16"),
    "bv": ("sbuf", [128, 64], "bfloat16"),
    "A": ("sbuf", [128, 1024], "bfloat16"), "B": ("sbuf", [128, 1024], "bfloat16"),
    "lastw": ("sbuf", [128, 4], "uint16"),
    "LF": ("sbuf", [128, 64], "uint16"),
    "hle": ("sbuf", [128, 64], "bfloat16"), "hli": ("sbuf", [128, 16], "uint16"),
    "yb": ("sbuf", [128, 1024], "bfloat16"),
}
for _k in range(10):
    SCRATCH["W%d" % _k] = ("sbuf", [128, BASE + 1024], "bfloat16")
    SCRATCH["L%d" % _k] = ("sbuf", [128, 64], "uint16")
for _k in range(8):
    SCRATCH["V%d" % _k] = ("sbuf", [128, 448], "bfloat16")
    SCRATCH["P%d" % _k] = ("sbuf", [128, 320], "bfloat16")
    SCRATCH["C%d" % _k] = ("sbuf", [128, 16], "uint16")
    SCRATCH["T%d" % _k] = ("sbuf", [128, 16], "uint16")
    SCRATCH["ps%d" % _k] = ("psum", [128, 512], "float32")
SEMAPHORES = ["v", "s", "pe", "gi", "dln", "dds", "dle", "dr", "dy", "loc", "le", "hle", "hli"] + ["ar%d" % k for k in range(8)]


def bits(engines):
    return sum(1 << e for e in engines)


def routes(rank, T, topo):
    src = T.cores[rank]
    later = list(range(len(T.cores) - 1, rank, -1))
    straight = [r for r in later if topo.may_write(src, T.cores[r])]
    cross = [r for r in later if r not in straight]
    if not cross:
        return straight, []
    able = [h for h in topo.cores_of(src) if h != src and T.rank_of(h) is None and topo.may_write(h, T.cores[cross[0]])]
    able.sort(key=lambda h: (topo.die(h) != topo.die(src), h))
    n = min(2, len(cross), len(able))
    return straight, [(able[i], cross[i::n], topo.engines(src, able[i])) for i in range(n)]


def runs(rank, T, topo):
    best = None
    for cut in range(1 << max(rank - 1, 0)):
        starts = [k for k in range(rank) if k == 0 or cut >> (k - 1) & 1]
        parts = list(zip(starts, starts[1:] + [rank]))
        if any(b - a > 3 for a, b in parts):
            continue
        calls = []
        for a, b in parts:
            come = [0 if topo.may_write(T.cores[k], T.cores[rank]) else LATE for k in range(a, b)]
            before = [("D", x, y - 1) for x, y in parts if y == a]
            if b - a > 1:
                calls += [(("P", a, k), [("P", a, k - 1)] if k > a else [], come[k - a]) for k in range(a, b)]
                calls += [(("C", a, b - 1), [("P", a, b - 1)], 0), (("D", a, b - 1), before + [("C", a, b - 1)], 0)]
            else:
                calls.append((("D", a, a), before, come[0]))
        end, order, now = {}, [], 0
        while calls:
            ready = [(max([now, c[2]] + [end[d] + (LIST if c[0][0] == "C" else 0) for d in c[1]]), c[0][0] == "D", c)
                     for c in calls if all(d in end for d in c[1])]
            t, _, c = min(ready)
            calls.remove(c)
            order.append(c[0])
            now = t + (0.25 if c[0][0] == "C" else 0.5)
            end[c[0]] = now + 0.5
        key = (max(end.values(), default=0), len(order))
        if best is None or key < best[0]:
            best = (key, order)
    return best[1]


def letters(k, rank, T, topo):
    a = min(c[1] for c in runs(rank, T, topo) if c[1] <= k <= c[2])
    return T["V%d" % a][:, 0:64] if a == k else T["V%d" % a][:, 256 + 64 * (k - a):320 + 64 * (k - a)]


def fan(g, T, topo, core, ranks, src, dst, rsem):
    ids = []
    for r in ranks:
        rid, pid = topo.addr(T.cores[r], core)
        ids.append(DstId(rid=rid, pnc=pid))
    g.remote_dma_fused([RemoteDMATransfer(dst_ids=ids, dma_engine_mask=topo.mask(core, T.cores[ranks[0]]), remote_sem=rsem,
                                          srcs=[src], dsts=[dst(r) for r in ranks])], local_sem=T.sem.loc)
    return len(topo.engines(core, T.cores[ranks[0]]))


def helper(g, core, T, topo):
    for r in range(len(T.cores)):
        if core not in topo.cores_of(T.cores[r]):
            continue
        for h, ranks, eng in routes(r, T, topo)[1]:
            if h != core:
                continue
            n = 0
            g.wait_ge(T.sem.hle, len(eng))
            n += fan(g, T, topo, core, ranks, T.hle[:, :], lambda d: letters(r, d, T, topo), T.sem.le)
            g.wait_ge(T.sem.hli, len(eng))
            for d in ranks:
                n += fan(g, T, topo, core, [d], T.hli[:, :], lambda d: T["T%d" % r][:, :], T.sem["ar%d" % r])
            g.wait_ge(T.sem.loc, n)


def rank_program(g, core, T, topo):
    rank = T.rank_of(core)
    if rank is None:
        helper(g, core, T, topo)
        return
    op = AluOpType
    fn = ActivationFunctionType
    V, S, PE, SY = g.vector, g.scalar, g.tensor, g.sync
    queue = {"v": V, "s": S, "pe": PE, "gi": g, "sy": SY}
    cnt = {}
    seen = {}

    def need(q, toks):
        top = {}
        for sem, val in toks:
            top[sem] = max(top.get(sem, 0), val)
        for sem in top:
            if seen.get((q, sem), 0) < top[sem]:
                queue[q].wait_ge(T.sem[sem], top[sem])
                seen[(q, sem)] = top[sem]

    def done(sem, ins, n=1):
        ins.then_inc(T.sem[sem], n)
        cnt[sem] = cnt.get(sem, 0) + n
        return (sem, cnt[sem])

    def gath(q, out, win, lst, deps):
        need(q, deps)
        if q == "v":
            return done("v", V.tensor_copy(out=out, in_=win.indirect(lst)))
        return done("s", S.activation(out=out, in_=win.indirect(lst), func=fn.Copy))

    def scan(out, data0, data1, initial, op0, op1, deps):
        need("v", deps)
        return done("v", V.tensor_tensor_scan(out=out, data0=data0, data1=data1, initial=initial, op0=op0, op1=op1))

    def ts(out, in0, s1, s2, op0, op1, deps):
        need("v", deps)
        if op1 is None:
            return done("v", V.tensor_scalar(out=out, in0=in0, scalar1=s1, scalar2=None, op0=op0))
        return done("v", V.tensor_scalar(out=out, in0=in0, scalar1=s1, scalar2=s2, op0=op0, op1=op1))

    def tt(out, in0, in1, op0, deps):
        need("v", deps)
        return done("v", V.tensor_tensor(out=out, in0=in0, in1=in1, op=op0))

    def act(out, in_, scale, bias, deps):
        need("s", deps)
        return done("s", S.activation(out=out, in_=in_, func=fn.Identity, bias=bias, scale=scale))

    def relist(out, pick, src, c0, c1, deps):
        need("pe", deps)
        for r in range(16):
            m = PE.matmul(out, pick(r), src[:, c0 + r:c1:16], r == 0, r == 15)
        return done("pe", m)

    mine = T["V%d" % rank]
    W = [T["W%d" % k] for k in range(10)]
    straight, relays = routes(rank, T, topo)
    last = not straight and not relays
    ln = done("dln", SY.dma_start(out=T.xl[:, :], in_=T.ln[:, :]), 16)
    ds = done("dds", S.dma_start(out=T.xd[:, :], in_=T.ds[:, :]), 16)
    le = done("dle", SY.dma_start(out=mine[:, 0:64], in_=T.le[:, :]), 16)
    flag = {"allow_small_or_imprecise_dtypes": True}
    ui = done("gi", g.iota(T.ui[:, :], [[1793, 2], [2048, 2], [256, 4]], 30976, -2048))
    one = done("v", V.memset(T.one[:, :], 1.0))
    need("gi", [one])
    y = done("gi", g.affine_select(T.Y[:, :], T.one[0:8, 0:144], [[1, 144]], op.is_equal, 0.0, -16, -16))
    ramp0 = done("gi", g.iota(T.ramp[:, 0:64], [[1, 64]], -64, 0, **flag))
    p64 = done("v", V.memset(T.pd[:, :], 0.0))
    uu = ts(T.uu[:, :], T.ui[:, :], 32767, None, op.bitwise_and, None, [ui])
    ramp = scan(T.ramp[:, 64:BASE], T.one[:, :], T.one[:, :], -1.0, op.mult, op.add, [one])
    mq = ts(T.mq[:, :], T.uu[:, :], 30720.0, 0.0, op.subtract, op.max, [uu])
    lo, run = T.mq[:, 8:9], T.mq[:, 12:13]
    lastf = scan(T.lastf[:, :], T.one[0:8, 0:64], T.xl[:, :], -1.0, op.add, op.add, [ln, one])
    p1 = relist(T.ps0[:, 0:4], lambda r: T.Y[:, 16 - r:144 - r], T.lastf, 0, 64, [lastf, y])
    need("v", [ds])
    pd = done("v", V.tensor_copy(out=T.pd[:, 0:64], in_=T.xd[:, :]))
    nd = act(T.pd[:, 72:136], T.xd[:, :], -1.0, 0.0, [ds, p64])
    need("pe", [pd, nd, ramp0])
    PE.matmul(T.ps1[:, 0:65], T.Y[:, 14:142], T.pd[:, 72:137], True, False)
    PE.matmul(T.ps1[:, 0:65], T.Y[:, 16:144], T.pd[:, 0:65], False, False)
    PE.matmul(T.ps1[:, 1:65], T.Y[:, 14:142], T.pd[:, 0:64], False, False)
    p2 = done("pe", PE.matmul(T.ps1[:, 1:65], T.Y[:, 15:143], T.ramp[0:8, 0:64], False, True))
    bg = []
    for j in (2, 3):
        bg.append(act(T.B[:, 256 * j:256 * j + 256], T.ramp[:, 64:BASE], lo, T.mq[:, j:j + 1], [mq, ramp]))
    for j in (0, 1):
        bg.append(ts(T.B[:, 256 * j:256 * j + 256], T.ramp[:, 64:BASE], lo, T.mq[:, j:j + 1], op.mult, op.add, [mq, ramp]))
    bv = act(T.bv[:, :], T.ps1[:, 1:65], 1.0, 0.0, [p2])
    zc = tt(T.col[:, 0:1], T.uu[:, 0:1], T.ui[:, 0:1], op.subtract, [uu])
    keep = [ts(T.A[:, 0:256], T.one[:, :], run, None, op.mult, None, [mq])]
    need("v", [p1])
    lw = done("v", V.tensor_copy(out=T.lastw[:, :], in_=T.ps0[:, 0:4]))
    keep.append(ts(T.A[:, 256:512], T.one[:, :], run, None, op.mult, None, [mq]))
    need("v", [lw, bv] + bg)
    sc = done("v", V.tensor_copy(out=T.B[:, :].indirect(T.lastw[:, 0:4]), in_=T.bv[:, :]))
    z = ts(T.Z[:, :], T.ramp[:, 49:193], 2048.0, T.col[:, 0:1], op.mult, op.is_equal, [zc, ramp0])
    h0 = scan(W[0][:, BASE:BASE + 512], T.A[:, 0:512], T.B[:, 0:512], T.ps1[:, 0:1], op.mult, op.add, [sc] + keep)
    root = {0: act(W[0][:, 0:BASE], T.ramp[:, :], lo, 0.0, [mq, ramp0])}
    h1 = scan(W[0][:, BASE + 512:BASE + 1024], T.A[:, 0:512], T.B[:, 512:1024], W[0][:, BASE + 511:BASE + 512],
              op.mult, op.add, [h0])
    need("gi", [root[0]])
    need("sy", [root[0]])
    for k in range(1, 8):
        if k < 8 - BYDMA:
            root[k] = done("gi", g.affine_select(W[k][:, 0:BASE], W[0][:, 0:BASE], [[0, BASE]], op.is_equal, 0.0, 0, 0))
        else:
            done("dr", SY.dma_start(out=W[k][:, 0:BASE], in_=W[0][:, 0:BASE]), 16)
            root[k] = ("dr", 16 * BYDMA)
    zero = done("gi", g.iota(T.V0[:, 64:320], [[0, 256]], 0, 0, **flag))

    span = {"A": (0, CUT), "B": (CUT, 768), "T": (768, 1024), "U": (CUT, 1024), "R": (0, 768), "W": (0, 1024),
            "P": (0, CUT // 2), "Q": (CUT // 2, CUT)}
    made = {0: [(0, 512, h0), (512, 1024, h1)]}
    lists = []
    bank = [2]
    free = {}
    pend = {}

    def after(where, a, b):
        return [x[-1] for x in where if x[0] < b and a < x[1]]

    def tolist(c, k, name):
        a, b = span[c]
        i = bank[0]
        bank[0] = 2 + (i - 1) % 6
        ps = T["ps%d" % i][:, 0:(b - a) // 16]
        t = relist(ps, lambda r: T.Z[:, 15 - r:143 - r], W[k], BASE + a, BASE + b, after(made[k], a, b) + [z] + free.get(i, []))
        pend[c] = (i, ps, name, t)

    def take(q, c, final):
        a, b = span[c]
        i, ps, k, t = pend.pop(c)
        buf = T.LF if final else T["L%d" % k]
        out = buf[:, a // 16:b // 16]
        if q == "v":
            t = ts(out, ps, 64.0, None, op.add, None, [t])
        else:
            t = act(out, ps, 1.0, 64.0, [t])
        free[i] = [t]
        lists.append((a, b, k, t))
        return t

    def jump(c, k, src, n):
        a, b = span[c]
        m = a + 32 * n if n is not None else (a + b) // 2
        for q, c0, c1 in (("s", m, b), ("v", a, m)):
            if c0 == c1:
                continue
            j = max(x[2] for x in lists if x[0] <= c0 < x[1])
            deps = [root[src]] + after([x for x in lists if x[2] == j], c0, c1) + after(made[src], 0, c1)
            t = gath(q, W[k][:, BASE + c0:BASE + c1], W[src][:, 0:BASE + c1], T["L%d" % j][:, c0 // 16:c1 // 16], deps)
            made.setdefault(k, []).append((c0, c1, t))

    final = []
    for w in (LAST if last else ORDER).split():
        if w[0] in "vs":
            t = take(w[0], w[1], w[-1] == "!")
            if w[-1] == "!":
                final.append(t)
                if w[1] == "T":
                    lt = t
        elif w[0] == "+":
            tolist(w[1], int(w[2]), int(w[-1]))
        else:
            k = int(w[1])
            jump(w[0], k, int(w[3]) if "@" in w else k - 1, int(w.split("/")[1]) if "/" in w else None)

    loc = 0
    for what in () if last else ("le", "list"):
        early = what == "le"
        need("gi", [le] if early else [lt])
        src = mine[:, 0:64] if early else T.LF[:, 48:64]
        if relays:
            ids = [DstId(rid=a[0], pnc=a[1]) for a in (topo.addr(h, core) for h, _, _ in relays)]
            g.remote_dma_fused([RemoteDMATransfer(dst_ids=ids, dma_engine_mask=bits(relays[0][2]), srcs=[src],
                                                  dsts=[T.hle[:, :] if early else T.hli[:, :] for _ in relays],
                                                  remote_sem=T.sem.hle if early else T.sem.hli)], local_sem=T.sem.loc)
            loc += len(relays[0][2])
        if straight:
            dst = (lambda d: letters(rank, d, T, topo)) if early else (lambda d: T["T%d" % rank][:, :])
            loc += fan(g, T, topo, core, straight, src, dst, T.sem.le if early else T.sem["ar%d" % rank])

    prev = [zero]
    total_le = 0
    got = []
    for k in range(rank):
        hop = [c for c in routes(k, T, topo)[1] if rank in c[1]]
        n = len(topo.engines(hop[0][0] if hop else T.cores[k], core))
        total_le += n
        got.append(("ar%d" % k, n))
    chain = runs(rank, T, topo)
    names = {}
    for what, a, k in chain:
        if what == "P" and k > a:
            names[k] = act(T["P%d" % k][:, 0:64], T.ramp[:, 64 * (k - a):64 * (k - a) + 64], lo, T.mq[:, 0:1], [])
    step = {}
    joined = [c for c in chain if c[0] == "C"]
    for what, a, k in chain:
        if what == "C":
            step[what, k] = [ts(T["C%d" % k][:, :], step["ps", k][0], 64.0, None, op.add, None, [step["ps", k][1]])]
            continue
        if what == "P":
            win, out, lst = (W[0] if k == a else T["P%d" % k])[:, 0:320], T["P%d" % (k + 1)], T["T%d" % k]
            deps = [got[k]] + ([root[0]] if k == a else [names[k]] + step["P", k - 1])
        else:
            win, out, lst = T["V%d" % a][:, 0:320 + 64 * (k - a)], T["V%d" % (k + 1)], T["C%d" % k if k > a else "T%d" % k]
            deps = prev + [("le", total_le)] + (step["C", k] if k > a else [got[k]])
        step[what, k] = [gath("v", out[:, 64:192], win, lst[:, 0:8], deps), gath("s", out[:, 192:320], win, lst[:, 8:16], deps)]
        if what == "D":
            prev = step[what, k]
        elif ("C", a, k) in chain:
            ps = T["ps%d" % joined.index(("C", a, k))][:, 0:16]
            step["ps", k] = (ps, relist(ps, lambda r: T.Z[:, 15 - r:143 - r], out, 64, 320, step[what, k]))

    win = mine[:, 0:320]
    deps = prev + [le] + final
    for a, b in zip(STORE, STORE[1:]):
        m = (a + b) // 64 * 32
        need("sy", [gath(q, T.yb[:, c0:c1], win, T.LF[:, c0 // 16:c1 // 16], deps) for q, c0, c1 in (("v", a, m), ("s", m, b))])
        done("dy", SY.dma_start(out=T.y[:, a:b], in_=T.yb[:, a:b]), 16)
    need("sy", [(s, cnt[s]) for s in ("dy", "v", "s", "pe", "gi", "dln", "dds", "dle", "dr") if s in cnt])
    if loc:
        g.wait_ge(T.sem.loc, loc)
